import numpy as np, ml_dtypes
CORES = [48,51,52,55]
N = 4
import mx_ref
BF = ml_dtypes.bfloat16
def gentries(a):
    return np.ascontiguousarray(a.reshape(8, 16, -1).transpose(0, 2, 1)).reshape(8, -1)
def gtable(e):
    e = np.asarray(e); return np.ascontiguousarray(e.reshape(8, -1, 16).transpose(0, 2, 1)).reshape(128, -1).astype(np.int32)
def gcols(t, e):
    v = np.concatenate([t.reshape(8, 16, -1, 4), np.zeros((8, 16, 1, 4), BF)], axis=2)
    return np.ascontiguousarray(np.stack([v[g][:, e[g]] for g in range(8)])).reshape(128, -1)
def gpick(z, e):
    return np.concatenate([z[16 * g:16 * g + 16][:, e[g]] for g in range(8)])
def tile(rs):
    return np.stack(rs, axis=2).reshape(128, -1).astype(BF)
def pick(q, e):
    c = np.concatenate([q[0].reshape(128, -1, 4), np.zeros((128, 1, 4), np.uint8)], axis=1); s = np.concatenate([q[1], np.ones((16, 1), np.uint8)], axis=1)
    return (np.ascontiguousarray(c[:, e].reshape(128, -1)), np.ascontiguousarray(s[:, e]))
def join(*qs):
    return (np.concatenate([q[0] for q in qs], axis=1), np.concatenate([q[1] for q in qs], axis=1))
def put(q, e, v):
    c, s = q[0].reshape(128, -1, 4).copy(), q[1].copy(); c[:, e] = v[0].reshape(128, -1, 4); s[:, e] = v[1]
    return (c.reshape(128, -1), s)
def pk(c, s):
    return (np.ascontiguousarray(c), mx_ref.live(s))
def emit(q):
    return q[0], q[1]
def packed(v, rng):
    q = [mx_ref.quantize(np.ascontiguousarray(v[r])) for r in range(N)]
    return np.stack([a for a, b in q]), np.stack([mx_ref.plane(b, rng) for a, b in q])
def values_of_codes():
    e, c = np.zeros((128, 128, 4), np.float32), np.zeros((128, 2, 4), np.uint8)
    e[np.arange(128), np.arange(128), 0] = 1
    c[:127, :, 0] = np.arange(256).reshape(2, 128).T[:127]
    return mx_ref.matmul(mx_ref.quantize(e.reshape(128, 512).astype(BF)), (c.reshape(128, 8), np.full((16, 2), 127, np.uint8))).T.reshape(-1).astype(np.float64)
CODE_VALUE, SCALE_VALUE = values_of_codes(), 2.0 ** (np.arange(256) - 127.0)
def decode(q):
    return (CODE_VALUE[q[0]].reshape(16, 8, -1, 4) * SCALE_VALUE[q[1]][:, None, :, None] + 0.0).reshape(128, -1).astype(np.float32)
def f(rng, *shape):
    return mx_ref.flush((rng.standard_normal(shape, dtype=np.float32) * np.exp2(rng.integers(-2, 3, shape[:-1] + (1,)))).astype(BF))
def wide(rng, *shape, cols=0):
    v = rng.standard_normal(shape, dtype=np.float32) * np.exp2(rng.integers(-12, 13, shape)).astype(np.float32)
    if cols: v *= np.repeat(np.exp2(rng.integers(-cols, cols + 1, shape[:-2] + (1, shape[-1] // 4))) * (rng.random(shape[:-2] + (1, shape[-1] // 4)) > 0.0625), 4, axis=-1).astype(np.float32)
    return mx_ref.flush(v.astype(BF))
C, K, P, R = 512, 128, 256, 2
def numbers_of(rng):
    return {"x": np.array(f(rng, N, 128, 4 * C)), "u": np.array(f(rng, N, 128, 512)), "v": np.array(f(rng, N, 128, 512))}
def mixed(rng):
    return rng.permuted(np.tile(np.arange(C), (N, 8, 1)), axis=2)
def links(e):
    return np.stack([gtable(e[r]) for r in range(N)])
def packedw(rng, w):
    c, p = packed(np.ascontiguousarray(w).reshape(N, 128, 2048), rng)
    return {"wc": c, "ws": p}
def weights(rng, still=()):
    w = np.array(f(rng, N, 128, 2048)).reshape(N, 8, 16, 4, 8, 16, 4)
    for i in still:
        w[:, :, i] = 0
        w[:, :, :, :, :, i] = 0
    return packedw(rng, w)
def setup_inputs(rng):
    return {**numbers_of(rng), "link": links(mixed(rng)), **weights(rng)}
def setup_inputs_ties(rng):
    d = numbers_of(rng)
    e = rng.permutation(N)
    x = d["x"].reshape(N, 8, 16, C, 4)
    for r in range(N):
        k = rng.permutation(C) % 3
        if r == e[0]: k = np.zeros(C, int)
        elif r in e[2::2]: k = rng.permutation(3)[np.arange(C) % 3]
        a = x[r][:, :8, :3].copy()
        a[:, :, 2] = 0
        x[r][:, :8] = a[:, :, k]
    x[e[1]] = 0
    u = d["u"].reshape(N, 8, 16, 128, 4)
    u[:, :, 8:, ::16] = 0
    u[:, :, 8:, 1::16] = 0
    t = mixed(rng)
    t[e[2]] = np.arange(C)
    t[e[3]] = t[e[3], :1].copy()
    return {"x": x.reshape(N, 128, 4 * C), "u": u.reshape(N, 128, 512), "v": d["v"], "link": links(t), **weights(rng, range(8))}
def setup_inputs_near(rng):
    d = numbers_of(rng)
    x = d["x"].astype(np.float32).reshape(N, 8, 16, C, 4)
    x[:, :, 0] = 0
    x[:, :, 8:] = 0
    u = d["u"].reshape(N, 128, 128, 4)
    u[:, :, ::16] = 0
    u[:, :, 1::16] = 0
    o = rng.permutation(N) % 4
    s = rng.integers(0, 256, (N, 8, C))
    for r in range(N):
        low = 2.0 ** -29 if o[r] == 3 else 2.0 ** -23
        for i in range(2): x[r, :, 8 + i] = ((s[r][:, :, None] >> (4 * i + np.arange(4))) & 1) * np.exp2(4.0 * i + np.arange(4)) * low
        x[r, :, 12, :, 0] = rng.integers(-1, 2, (8, C)) * (2.0 ** -29 if o[r] == 3 else 2.0 ** -20)
        if o[r] == 3: x[r, :, 13, :, 0] = x[r, :, 12, :, 0]
        if o[r] < 2:
            x[r, :, 0, :, 0] = rng.integers(0, 2, (8, C)) * 2.0 - 1.0
            x[r, :, 11, :, 0] = 2.0 ** -10
        if o[r] == 2:
            for g in range(8): x[r, g, 0, rng.permutation(C)[:2], 0] = np.array([1.0, -1.0])
        for g in rng.permutation(8)[:4]: x[r, g, 12, rng.integers(C), 0] = 2.0 ** 29 * rng.choice([-1.0, 1.0])
        k = 1.0 if o[r] == 0 else 2.0 ** -30
        for h in range(0, 128, 16):
            if o[r] < 2:
                u[r, h, h, 0] = k
                u[r, h + 11, h, 0] = k
            if o[r] == 2: u[r, h, h, 0] = 1.0
            u[r, h + 8, h] = k
            u[r, h + 9, h] = k
            u[r, h + 12, h + 1, 0] = 1.125 * 2.0 ** -30 if o[r] == 3 else 2.0 ** -30
            if o[r] == 3: u[r, h + 13, h + 1, 0] = -1.0 * 2.0 ** -30
    return {"x": x.reshape(N, 128, 4 * C).astype(BF), "u": u.reshape(N, 128, 512), "v": d["v"], "link": links(mixed(rng)), **weights(rng, [0, 8, 9, 10, 11, 12, 13, 14, 15])}
def setup_inputs_caps(rng):
    d = numbers_of(rng)
    x = np.zeros((N, 8, 16, C, 4))
    z = (N, 8, 8, C, 4)
    x[:, :, :8] = rng.choice([-1.0, 1.0], z) * (1.0 + (2 * rng.integers(0, 64, z) + 1) * 2.0 ** -7) * np.exp2(-1.0 * rng.integers(8, 15, z))
    x[:, :, 0, :, 0] = rng.choice([1.96875, 1.84375], (N, 8, C))
    s = mixed(rng)
    for i in range(3): x[:, :, 8 + i] = ((s[:, :, :, None] >> (4 * i + np.arange(4))) & 1) * np.exp2(4.0 * i + np.arange(4))
    side = rng.permutation(N) % 2 * 2 - 1
    q = np.argsort(-s * side[:, None, None], axis=2)[:, :, 1::2]
    one = rng.random((N, 8, C)) < 0.5
    a = rng.permutation(8)
    for i in range(6):
        g, t, k = a[i], i % R, 0
        for r in range(N):
            if (r >> t) & 1: one[r, g] = True
            else:
                n = K if i < 3 else K - 1 + 2 * (k % 2)
                k += 1
                one[r, g, q[r, g]] = rng.permutation(P) < n
    one[:, a[6]] = (((np.arange(N) >> (R - 1)) & 1) == 1)[:, None]
    one[:, a[7]] = ((np.arange(N) & 1) == 1)[:, None]
    x[:, :, 12, :, 0] = np.where(one, 1.0, -1.0 * rng.integers(0, 2, (N, 8, C)))
    u = d["u"].reshape(N, 128, 128, 4)
    u[:, :, ::16] = 0
    u[:, :, 1::16] = 0
    for r in range(N):
        for h in range(0, 128, 16):
            u[r, h + 8:h + 11, h] = float(side[r])
            u[r, h + 12, h + 1, 0] = 1.0
    return {"x": x.astype(np.float32).reshape(N, 128, 4 * C).astype(BF), "u": u.reshape(N, 128, 512), "v": d["v"], "link": links(mixed(rng)), **weights(rng, range(8, 16))}
def setup_inputs_huge(rng):
    d = numbers_of(rng)
    o = rng.permutation(N)
    c = rng.integers(0, 2, (N, 1, 1, C, 1)) * 2.0 - 1.0
    c[:, :, :, :2] = np.array([1.0, -1.0])[:, None]
    c[o == 1] = -1.0
    c[o == 2] = 1.0
    x = 0.6 + 0.09 * rng.random((N, 8, 16, C, 4))
    x[o == 0] = np.where(rng.random((1, 8, 16, C, 4)) < 0.125, 0.8125, 0.875)
    u = d["u"].reshape(N, 128, 128, 4)
    for i in range(2):
        a = 2.0 ** 29 * (1.0 - 0.1 * rng.random((N, 128, 8, 4)))
        a[o == 0] = 2.0 ** 30 * np.where(rng.random((1, 128, 8, 4)) < 0.03125, 0.875, 1.0)
        turned = (o % 2 == 1) if i else (o == 0) | (o > N // 2)
        for r in range(N):
            if turned[r]: a[r] *= (rng.permutation(8) % 2 * 2.0 - 1.0)[None, :, None]
        u[:, :, i::16] = a.astype(np.float32).astype(BF)
    w = np.zeros((N, 128, 4, 128, 4), np.float32)
    i = np.arange(128)
    for b in range(4): w[:, i, b, i, b] = 1
    return {"x": (2.0 ** 30 * x * c).astype(np.float32).reshape(N, 128, 4 * C).astype(BF), "u": u.reshape(N, 128, 512), "v": d["v"], "link": links(mixed(rng)), **packedw(rng, w.astype(BF))}
def setup_inputs_spread(rng):
    d = setup_inputs(rng)
    d["x"] = wide(rng, N, 128, 4 * C, cols=6)
    return d
def check_inputs(d):
    b = []
    for k in ("x", "u", "v"):
        a = np.abs(d[k].astype(np.float32))
        if not (np.isfinite(a).all() and ((a == 0) | (a >= 2.0 ** -30) & (a <= 2.0 ** 30)).all()): b.append("a value of " + k)
    none, least, most = [emit(mx_ref.quantize(np.full((128, 16), k, np.float32).astype(BF)))[1][0, 0] for k in (0.0, 2.0 ** -30, 2.0 ** 30)]
    for r in range(N):
        if (np.sort(gentries(d["link"][r]), axis=1) != np.arange(C)).any(): b.append("link: a group's entries are no permutation")
        if ((d["wc"][r] == 0x7F) | (d["wc"][r] == 0xFF)).any(): b.append("wc: a code that is no number")
        s = mx_ref.live(d["ws"][r])
        if ((s != none) & ((s < least) | (s > most))).any(): b.append("ws: a scale out of range")
    return b
def at(a, e):
    return np.take_along_axis(a, e, axis=1)
def reference(x, u, v, link, wc, ws):
    qu = [mx_ref.quantize(u[r]) for r in range(N)]
    lay = [pk(wc[r], ws[r]) for r in range(N)]
    now = [x[r] for r in range(N)]
    to = [gentries(link[r]) for r in range(N)]
    for t in range(R):
        d = 2 ** t
        own, order, bit = [], [], []
        for r in range(N):
            q = mx_ref.quantize(now[r])
            own.append(decode(q))
            s = mx_ref.matmul(qu[r], q)
            order.append(np.argsort(-(s[::16] + np.float32(0.0)), axis=1, kind="stable"))
            bit.append(s[1::16] > 0)
        kept, names, left, places, turned = [], [], [], [], []
        for r in range(N):
            k, q = order[r][:, 0::2], order[r][:, 1::2]
            there = at(to[r], q)
            fails = at(bit[r], q) != at(bit[(r + d) % N], there)
            j = np.argsort(fails.astype(np.int64), axis=1, kind="stable")
            k, q, there = at(k, j), at(q, j), at(there, j)
            h = own[r].astype(BF)
            a = ((gcols(h, k).astype(np.float32) + gcols(h, q).astype(np.float32)) * np.float32(0.5)).astype(BF)
            kept.append(mx_ref.quantize(np.ascontiguousarray(a[:, :4 * K])))
            left.append(mx_ref.quantize(np.ascontiguousarray(a[:, 4 * K:])))
            names.append(there[:, :K])
            places.append(q[:, K:])
            m = np.tile(np.arange(C), (8, 1))
            np.put_along_axis(m, k[:, K:], q[:, K:], axis=1)
            np.put_along_axis(m, q[:, K:], k[:, K:], axis=1)
            turned.append(at(to[r], m))
        to = [at(turned[(r + d) % N], to[r]) for r in range(N)]
        for r in range(N):
            c = (r - d) % N
            slots = join(kept[c], left[r])
            e = np.full((8, C), P)
            np.put_along_axis(e, places[r], np.tile(np.arange(K, P), (8, 1)), axis=1)
            np.put_along_axis(e, names[c], np.tile(np.arange(K), (8, 1)), axis=1)
            made = []
            for b in range(4):
                h = mx_ref.matmul(pick(lay[r], np.arange(128 * b, 128 * b + 128)), slots)
                h = np.concatenate([h, np.zeros((128, 1), np.float32)], axis=1)
                made.append(gpick(h, e) * np.float32(0.03125) + own[r][:, b::4])
            now[r] = tile(made)
    y, lk = np.zeros((N, 128, C), np.float32), np.zeros((N, 8, C), np.float32)
    oc, osc = np.zeros((N, 128, 4 * C), np.uint8), np.zeros((N, 16, C), np.uint8)
    for r in range(N):
        q = mx_ref.quantize(now[r])
        y[r] = mx_ref.matmul(mx_ref.quantize(v[r]), q)
        lk[r] = to[r]
        oc[r], osc[r] = emit(q)
    return {"y": y, "lk": lk, "oc": oc, "osc": osc}

@@ -1,0 +1,388 @@
+from concourse.mybir import dt, AluOpType as OP, ActivationFunctionType as AF
+
+N, ROUNDS = 4, 2
+HW = 264
+BIG = 2.0 ** 14
+TC = [max(128, 64 * (k + 1)) for k in range(8)]
+TO = [sum(TC[:k]) for k in range(9)]
+CODES, F32, BF = "float8_e4m3fn_x4", "float32", "bfloat16"
+
+SCRATCH = {}
+
+
+def buf(names, cols, dtype, where="sbuf"):
+    for n in names.split(): SCRATCH[n] = (where, [128, cols], dtype)
+
+
+buf("X0 XN0 XN1 EB FH FB", 2048, BF)
+buf("UB VB ON OB BR0 BR1 TB0 TB1 AK0 AK1 AL0 AL1", 512, BF)
+buf("UQ UR UT VQ OQ AKQ0 AKQ1 ALQ0 ALQ1 INQ0 INQ1", 128, CODES)
+buf("UQS URS UTS VQS OQS AKS0 AKS1 ALS0 ALS1 INS0 INS1", 128, "uint8")
+buf("WQ EQ", 512, CODES)
+buf("WS EQS", 512, "uint8")
+buf("XQ", 512 * 3, CODES)
+buf("XS", 512 * 3, "uint8")
+buf("QT", TO[8], CODES)
+buf("QS", TO[8], "uint8")
+buf("BT", 4 * TO[8], BF)
+buf("JUNK", 8448, BF)
+buf("KB", 1024, BF)
+buf("LINKI", 32, "int32")
+buf("CA", 2560, F32)
+buf("CB", 2816, F32)
+buf("SM", 64, F32)
+buf("INT", 20, "int32")
+buf("UO", 16, "uint16")
+buf("W3", 1536, F32)
+buf("RS", 32, F32)
+buf("WK", 128, F32)
+buf("EX", 2432, F32)
+buf("II", 48, "int32")
+buf("U16", 80, "uint16")
+buf("OWS PAY POS POSA FO EW YS LR0 LR1 TR0 TR1 TRW0 TRW1", 512, F32)
+buf("FF", 1024, F32)
+buf("NMR", 128, F32)
+buf("LQK0 LQK1", 256, F32)
+buf("HS", 4 * HW, F32)
+buf("KQ0 KQ1 LL0 LL1", 32, "uint16")
+buf("NL0 NL1 NLI0 NLI1", 8, "uint16")
+buf("TRD0 TRD1 TRX0 TRX1", 32, F32, "dram")
+buf("BRD0 BRD1 BRX0 BRX1", 32, BF, "dram")
+buf("P0 P1 P2 P3 P4 P5 P6 P7", 512, F32, "psum")
+
+PIECE = {
+    "AROW": ("CA", 0, 512), "M1": ("CA", 512, 512), "ML": ("CA", 1024, 512), "MX": ("CA", 1536, 512), "CR": ("CA", 2048, 512),
+    "IOTA": ("CB", 0, 512), "I4": ("CB", 512, 512), "CXA": ("CB", 1024, 512), "CXB": ("CB", 1536, 512), "CX": ("CB", 2048, 512), "ONEF": ("CB", 2560, 256),
+    "PM": ("SM", 0, 2), "PN": ("SM", 2, 2), "MC": ("SM", 4, 2), "B0": ("SM", 6, 1), "B1": ("SM", 7, 1), "R5": ("SM", 8, 32), "J16": ("SM", 40, 16),
+    "UOI": ("INT", 0, 16), "PI": ("INT", 16, 2), "PJ": ("INT", 18, 2),
+    "MSK": ("W3", 0, 512), "SCN": ("W3", 512, 512), "SBD": ("W3", 1024, 512),
+    "RSI": ("WK", 0, 32), "RK": ("WK", 32, 32), "NX1": ("WK", 64, 16), "NX2": ("WK", 80, 16), "NN": ("WK", 96, 16), "TOT": ("WK", 112, 1),
+    "EXA": ("EX", 0, 512), "EXB": ("EX", 512, 256), "EXK": ("EX", 768, 512), "EXN": ("EX", 1280, 128), "EXE": ("EX", 1408, 512), "EXL": ("EX", 1920, 512),
+    "CSL": ("II", 0, 32), "VL": ("II", 32, 16),
+    "RKU": ("U16", 0, 32), "NU": ("U16", 32, 16), "EL": ("U16", 48, 32),
+    "FR": ("FF", 0, 256), "F5": ("FF", 256, 256), "FC": ("FF", 512, 256), "VP": ("FF", 768, 256),
+}
+SEMAPHORES = ["cv", "cs", "ct", "cg", "ldx0", "ldx1", "ldu", "ldk", "ldv", "ldw", "st"]
+for _t in range(ROUNDS):
+    SEMAPHORES += [s + "%d" % _t for s in ("bro", "bra", "brl", "tbx", "nma", "nml", "cda", "cdl", "tro", "tra", "trl", "trx")]
+
+
+def rank_program(g, core, T, topo):
+    rank = T.rank_of(core)
+    if rank is None:
+        return
+    queue = {"v": g.vector, "s": g.scalar, "t": g.tensor, "g": g, "y": g.sync}
+    own = {"v": "cv", "s": "cs", "t": "ct", "g": "cg"}
+    count = {"cv": 0, "cs": 0, "ct": 0, "cg": 0}
+    total = {}
+    know = {q: {} for q in queue}
+    wrote, read = {}, {}
+
+    def w(n, a=0, b=None, step=1):
+        if n in PIECE: name, off, width = PIECE[n]
+        else: name, off, width = n, 0, SCRATCH[n][1][1]
+        if b is None: b = width
+        if step == 1: return T[name][:, off + a:off + b]
+        return T[name][:, off + a:off + b:step]
+
+    def settle(q, reads, writes):
+        need = []
+        for k in reads:
+            if k in wrote: need.append(wrote[k])
+            if k[0] == "P" and k[1:].isdigit():
+                need += [r for r in read.get(k, []) if r[0] != q]
+        for k in writes:
+            if k in wrote: need.append(wrote[k])
+            need += [r for r in read.get(k, []) if r[0] != q or r[1] not in count]
+        need.sort(key=lambda n: -n[2])
+        for _, sem, val, seen in need:
+            if know[q].get(sem, 0) >= val: continue
+            queue[q].wait_ge(T.sem[sem], val)
+            know[q][sem] = val
+            for s2 in seen: know[q][s2] = max(know[q].get(s2, 0), seen[s2])
+
+    def note(token, reads, writes):
+        for k in reads: read.setdefault(k, []).append(token)
+        for k in writes:
+            wrote[k] = token
+            read[k] = []
+
+    def op(q, call, reads, writes):
+        settle(q, reads, writes)
+        sem = own[q]
+        call().then_inc(T.sem[sem], 1)
+        count[sem] += 1
+        total[sem] = count[sem]
+        note((q, sem, count[sem], dict(know[q])), reads, writes)
+
+    def dma(q, out, in_, sem, of, reads, writes):
+        settle(q, reads, writes)
+        queue[q].dma_start(out, in_).then_inc(T.sem[sem], 16)
+        total[sem] = 16 * of
+        note((q, sem, 16 * of, dict(know[q])), reads, writes)
+
+    def send(dst, out, in_, rsem, lsem, reads, of=1):
+        settle("g", reads, [])
+        rid, pid = topo.addr(dst)[:2]
+        n = len(topo.engines(core, dst))
+        g.remote_dma(out, in_, T.sem[rsem], T.sem[lsem], pid, rid, topo.mask(core, dst))
+        total[lsem] = n * of
+        note(("g", lsem, n * of, dict(know["g"])), reads, [])
+
+    def lands(src, key, rsem, of=1):
+        n = len(topo.engines(src, core)) * of
+        total[rsem] = n
+        note(("far", rsem, n, {}), [], [key])
+
+    V, S, G = g.vector, g.scalar, g
+
+    def ts(out, in0, a, b, op0, op1, reads, writes):
+        if op1 is None: op("v", lambda: V.tensor_scalar(out, in0, a, None, op0), reads, writes)
+        else: op("v", lambda: V.tensor_scalar(out, in0, a, b, op0, op1), reads, writes)
+
+    def tt(out, in0, in1, o, reads, writes): op("v", lambda: V.tensor_tensor(out, in0, in1, o), reads, writes)
+    def cp(out, in_, reads, writes): op("v", lambda: V.tensor_copy(out, in_), reads, writes)
+    def fill(out, c, writes): op("v", lambda: V.memset(out, c), [], writes)
+    def act(out, in_, func, scale, reads, writes): op("s", lambda: S.activation(out, in_, func, scale=scale), reads, writes)
+    def scan(out, d0, d1, reads, writes): op("v", lambda: V.tensor_tensor_scan(out, d0, d1, 0.0, OP.mult, OP.add), reads, writes)
+    def quant(q, s, in_, reads, writes): op("v", lambda: V.quantize_mx(q, s, in_), reads, writes)
+    def mm(out, a, asc, b, bsc, start, stop, reads, writes): op("t", lambda: g.tensor.matmul_mx(out, a, asc, b, bsc, start, stop), reads, writes)
+
+    def lift(ex, a, row, n, key):
+        scan(w(ex, a, a + n), w("CX", 0, n), row, ["CX", key], ["%s.%d" % (ex, a)])
+
+    def down(out, ex, a, n, bias, key):
+        ts(out, w(ex, a + 15, a + n, 16), w("MC", 0, 1), w(bias), OP.mult, OP.add, ["%s.%d" % (ex, a), "MC", bias], [key])
+
+    dma("s", w("UB"), T.u[:, :], "ldu", 1, [], ["UB"])
+    dma("y", w("X0", 0, 1024), T.x[:, 0:1024], "ldx0", 1, [], ["X0a"])
+    dma("s", w("X0", 1024, 2048), T.x[:, 1024:2048], "ldx1", 1, [], ["X0b"])
+    dma("y", w("LINKI"), T.link[:, :], "ldk", 1, [], ["LINKI"])
+    dma("y", w("WQ").bitcast(dt.uint8), T.wc[:, :], "ldw", 2, [], ["WQ"])
+    dma("y", w("WS"), T.ws[:, :], "ldw", 2, [], ["WS"])
+    dma("y", w("VB"), T.v[:, :], "ldv", 1, [], ["VB"])
+
+    def iota(n, a, b, pattern, base, cm):
+        out = w(n, a, b)
+        if n in ("UOI", "PI"): op("g", lambda: G.iota(out, pattern, base, cm), [], [n])
+        else: op("g", lambda: G.iota(out, pattern, base, cm, allow_small_or_imprecise_dtypes=True), [], [n])
+
+    iota("UOI", 0, 16, [[1, 2], [16, 8]], 0, 0)
+    iota("PI", 0, 2, [[0, 2]], 0, 1)
+    iota("AROW", 0, 512, [[0, 32], [1, 16]], 0, 0)
+    fill(w("ON"), 1.0, ["ON"])
+    fill(w("EB"), 0.0, ["EB"])
+    ts(w("PJ"), w("PI"), 15, None, OP.bitwise_and, None, ["PI"], ["PJ"])
+    cp(w("UO"), w("UOI"), ["UOI"], ["UO"])
+    cp(w("PM"), w("PJ"), ["PJ"], ["PM"])
+    pm = w("PM", 0, 1)
+    ts(w("ML"), w("AROW"), pm, 2e25, OP.is_lt, OP.mult, ["AROW", "PM"], ["ML"])
+    ts(w("M1"), w("AROW"), pm, None, OP.is_equal, None, ["AROW", "PM"], ["M1"])
+    ts(w("CR"), w("AROW"), 0.0, None, OP.is_gt, None, ["AROW"], ["CR"])
+    op("s", lambda: S.activation(w("MX"), w("ML"), AF.Copy, bias=-1e25, scale=1.0), ["ML"], ["MX"])
+    for b in range(4):
+        op("g", lambda b=b: G.affine_select(w("EB", 512 * b + b, 512 * b + 512, 4), w("ON", 0, 128), [[-1, 128]], OP.is_equal, 0.0, 0, 1), ["ON", "EB"], ["EB%d" % b])
+    op("g", lambda: G.affine_select(w("OB"), w("ON"), [[-16, 8], [0, 64]], OP.is_ge, 0.0, 0, 1), ["ON"], ["OB"])
+    op("g", lambda: G.affine_select(w("OB"), w("OB"), [[16, 8], [0, 64]], OP.is_ge, 0.0, 15, -1), ["OB"], ["OB"])
+    iota("IOTA", 0, 512, [[1, 512]], 0, 0)
+    iota("I4", 0, 512, [[4, 512]], 4, 0)
+    iota("R5", 0, 32, [[-16, 32]], 511, 0)
+    iota("J16", 0, 16, [[16, 16]], 0, 0)
+    quant(w("UQ"), w("UQS"), w("UB"), ["UB"], ["UQ"])
+    for k in range(8):
+        fill(w("BT", 4 * TO[k] + 256 * k, 4 * TO[k + 1]), 0.0, ["BT%d.%d%s" % (k, s, h) for s in range(4) for h in "ad"])
+    for q, o in (("UR", 0), ("UT", 8)):
+        cp(w(q).bitcast(dt.uint32), w("UQ").bitcast(dt.uint32).indirect(w("UO", o, o + 8)), ["UQ", "UO"], [q])
+        cp(w(q + "S"), w("UQS").indirect(w("UO", o, o + 8)), ["UQ", "UO"], [q + "S"])
+
+    def late_constants():
+        quant(w("EQ"), w("EQS"), w("EB"), ["EB%d" % b for b in range(4)] + ["EB"], ["EQ"])
+        quant(w("OQ"), w("OQS"), w("OB"), ["OB"], ["OQ"])
+        cp(w("LL0"), w("LINKI"), ["LINKI"], ["LL0"])
+        ts(w("PN"), w("PM"), 1.0, None, OP.add, None, ["PM"], ["PN"])
+
+    def later_constants():
+        ts(w("CXA"), w("AROW"), pm, None, OP.is_gt, None, ["AROW", "PM"], ["CXA"])
+        ts(w("CXB"), w("AROW"), w("PN", 0, 1), BIG - 1.0, OP.is_equal, OP.mult, ["AROW", "PN"], ["CXB"])
+        ts(w("MC"), w("PM"), 15.0, 1.0 - 1.0 / BIG, OP.is_equal, OP.mult, ["PM"], ["MC"])
+        tt(w("CX"), w("CXA"), w("CXB"), OP.add, ["CXA", "CXB"], ["CX"])
+        ts(w("B0"), pm, 15.0, -0.468, OP.is_lt, OP.mult, ["PM"], ["B0"])
+        ts(w("R5"), w("R5"), pm, None, OP.subtract, None, ["R5", "PM"], ["R5"])
+        ts(w("MC"), w("MC"), 1.0 / BIG, None, OP.add, None, ["MC"], ["MC"])
+        ts(w("B1"), w("B0"), 1.0, None, OP.subtract, None, ["B0"], ["B1"])
+        ts(w("J16"), w("J16"), pm, None, OP.add, None, ["J16", "PM"], ["J16"])
+        fill(w("ONEF"), 1.0, ["ONEF"])
+        fill(w("HS"), 0.0, ["HS%d%s" % (b, h) for b in range(4) for h in "KL"] + ["HSZ"])
+        quant(w("VQ"), w("VQS"), w("VB"), ["VB"], ["VQ"])
+        fill(w("TRW1"), 0.0, ["TRW1"])
+
+    def turn_rows(t):
+        n, lr = "LQK%d" % t, "LR%d" % t
+        act(w(n, 0, 128), w(lr).indirect(w("KQ%d" % t, 24, 32)), AF.Copy, 1.0, [lr, "QL%d" % t], [n + "a"])
+        act(w(n, 128, 256), w(lr).indirect(w("KQ%d" % t, 16, 24)), AF.Copy, 1.0, [lr, "KL%d" % t], [n + "b"])
+
+    def turn_send(t, back):
+        n, tr = "LQK%d" % t, "TR%d" % t
+        cp(w(tr).indirect(w("KQ%d" % t, 16, 32)), w(n), [n + "a", n + "b", "QL%d" % t, "KL%d" % t], [tr])
+        dma("y", w("TRD%d" % t), T[tr][0:128:16, :], "tro%d" % t, 1, [tr], ["TRD%d" % t])
+        send(back, w("TRX%d" % t), w("TRD%d" % t), "tra%d" % t, "trl%d" % t, ["TRD%d" % t])
+
+    def spread(n, src, key, sem):
+        for a in range(16): dma("y", T[n][a:128:16, :], w(src), sem, 16, [src], ["%s.%d" % (n, a)])
+
+    for t in range(ROUNDS):
+        d = 2 ** t
+        nxt, prv = T.cores[(rank + d) % N], T.cores[(rank - d) % N]
+        last = t == ROUNDS - 1
+        X, xk = ("X0", ["X0a", "X0b"]) if t == 0 else ("XN%d" % (t - 1), ["XN%d.%d" % (t - 1, b) for b in range(4)])
+        xq, xs = w("XQ", 512 * t, 512 * t + 512), w("XS", 512 * t, 512 * t + 512)
+        kx = "XQ%d" % t
+        ll, lr, kq, br, tb = ("%s%d" % (n, t) for n in ("LL", "LR", "KQ", "BR", "TB"))
+        quant(xq, xs, w(X), xk, [kx])
+        mm(w("P0"), w("UR"), w("URS"), xq, xs, True, True, ["UR", "URS", kx], ["P0"])
+        mm(w("P1"), w("UT"), w("UTS"), xq, xs, True, True, ["UT", "UTS", kx], ["P1"])
+        if t: turn_send(t - 1, T.cores[(rank - d // 2) % N])
+        tt(w("MSK"), w("P0"), w("M1"), OP.mult, ["P0", "M1"], ["MSK"])
+        ts(w(br), w("P1"), 0.0, 0.5, OP.is_gt, OP.subtract, ["P1"], [br])
+        scan(w("SCN"), w("CR"), w("MSK"), ["CR", "MSK"], ["SCN"])
+        tt(w("SBD"), w("P0"), w("MX"), OP.min, ["P0", "MX"], ["SBD"])
+        dma("y", w("BRD%d" % t), T[br][0:128:16, :], "bro%d" % t, 1, [br], ["BRD%d" % t])
+        send(prv, w("BRX%d" % t), w("BRD%d" % t), "bra%d" % t, "brl%d" % t, ["BRD%d" % t])
+        if t:
+            p = t - 1
+            lands(T.cores[(rank + d // 2) % N], "TRX%d" % p, "tra%d" % p)
+            spread("TRW%d" % p, "TRX%d" % p, "", "trx%d" % p)
+        lands(nxt, "BRX%d" % t, "bra%d" % t)
+        spread(tb, "BRX%d" % t, "", "tbx%d" % t)
+        if t == 0: late_constants()
+        for b in range(4):
+            mm(w("P%d" % (2 + b)), w("EQ", 128 * b, 128 * b + 128), w("EQS", 128 * b, 128 * b + 128), xq, xs, True, True, ["EQ", kx], ["P%d" % (2 + b)])
+
+        def colsum(k):
+            q, s = w("QT", TO[k], TO[k + 1]), w("QS", TO[k], TO[k + 1])
+            quant(q, s, w("BT", 4 * TO[k], 4 * TO[k + 1]), ["BT%d.%d%s" % (k, i, h) for i in range(4) for h in "ad"], ["QT%d" % k])
+            mm(w("P6", 0, TC[k]), w("OQ"), w("OQS"), q, s, k == 7, k == 0, ["OQ", "QT%d" % k], ["P6"])
+
+        for k in range(7, -1, -1):
+            o = 4 * TO[k]
+            for i in range(3, -1, -1):
+                c = 4 * k + i
+                key = "BT%d.%d" % (k, i)
+                sc = w("SCN", 16 * c + 15, 16 * c + 16)
+                if c: ts(w("BT", o + i, o + 64 * c, 4), w("P0", 0, 16 * c), sc, None, OP.is_ge, None, ["P0", "SCN"], [key + "a"])
+                ts(w("BT", o + 64 * c + i, o + 64 * c + 64, 4), w("SBD", 16 * c, 16 * c + 16), sc, None, OP.is_ge, None, ["SBD", "SCN"], [key + "d"])
+                j = 8 * c * (c + 1)
+                op("s", lambda: S.activation(w("JUNK", j, j + 16 * c + 16), w("BT", o + i, o + 64 * c + 64, 4), AF.Copy, accum_out=w("RS", c, c + 1)), [key + "a", key + "d"], ["JUNK%d" % c, "RS%d" % c])
+                if i == 3 and k < 7: colsum(k + 1)
+            if k == 6:
+                if t == 0: later_constants()
+                tt(w("OWS"), w(br), w("I4"), OP.mult, [br, "I4"], ["OWS"])
+            if k == 5 and t == 0: act(w(lr), w("IOTA").indirect(w(ll)), AF.Copy, 1.0, ["IOTA", ll], [lr])
+            if k == 3 and t: act(w(lr), w("TRW%d" % (t - 1)).indirect(w("LL%d" % (t - 1))), AF.Copy, 1.0, ["TRW%d.%d" % (t - 1, a) for a in range(16)] + ["LL%d" % (t - 1)], [lr])
+            if k == 1 and t: lift("EXL", 0, w(lr), 512, lr)
+        if t: down(w(ll), "EXL", 0, 512, "B0", ll)
+        colsum(0)
+        for b in range(4): act(w("FH", 512 * b, 512 * b + 512), w("P%d" % (2 + b)), AF.Copy, 0.5, ["P%d" % (2 + b)], ["FH%d" % b])
+        tt(w("PAY"), w(tb).indirect(w(ll)), w("OWS"), OP.mult, ["%s.%d" % (tb, a) for a in range(16)] + [ll, "OWS"], ["PAY"])
+        tt(w("RSI"), w("RS"), w("R5"), OP.add, ["RS%d" % c for c in range(32)] + ["R5"], ["RSI"])
+        lift("EXA", 0, w("P6"), 512, "P6")
+        down(w("CSL"), "EXA", 0, 512, "B0", "CSL")
+        tt(w("RK"), w("RSI"), w("CSL"), OP.subtract, ["RSI", "CSL"], ["RK"])
+        cp(w("RKU"), w("RK"), ["RK"], ["RKU"])
+        cp(w("POS").indirect(w("RKU")), w("PAY"), ["RKU", "PAY"], ["POS"])
+        act(w("POSA"), w("POS"), AF.Abs, 1.0, ["POS"], ["POSA"])
+        ts(w("FR"), w("POS", 1, 512, 2), 0.0, None, OP.is_lt, None, ["POS"], ["FR"])
+        ts(w("F5"), w("POS", 1, 512, 2), 0.0, 512.0, OP.is_lt, OP.mult, ["POS"], ["F5"])
+        scan(w("FC"), w("ONEF"), w("FR"), ["ONEF", "FR"], ["FC"])
+        fill(w("EW"), 256.0, ["EW"])
+        tt(w("VP"), w("FC"), w("F5"), OP.add, ["FC", "F5"], ["VP"])
+        ts(w("TOT"), w("FC", 255, 256), -1.0, -257.0, OP.mult, OP.add, ["FC"], ["TOT"])
+        lift("EXB", 0, w("VP"), 256, "VP")
+        down(w("VL"), "EXB", 0, 256, "B0", "VL")
+        tt(w("NX1"), w("J16"), w("VL"), OP.subtract, ["J16", "VL"], ["NX1"])
+        ts(w("NX2"), w("VL"), w("TOT"), None, OP.add, None, ["VL", "TOT"], ["NX2"])
+        tt(w("NN"), w("NX1"), w("NX2"), OP.max, ["NX1", "NX2"], ["NN"])
+        cp(w("NU"), w("NN"), ["NN"], ["NU"])
+        cp(w("FO", 0, 256).indirect(w("NU")), w("POSA", 0, 512, 2), ["NU", "POSA"], ["FOk"])
+        cp(w("FO", 256, 512).indirect(w("NU")), w("POSA", 1, 512, 2), ["NU", "POSA"], ["FOq"])
+        for b in range(4): act(w("FB", 512 * b, 512 * b + 512), w("P%d" % (2 + b)), AF.Copy, 1.0, ["P%d" % (2 + b)], ["FB%d" % b])
+
+        def lists(h):
+            o = 128 if h == "L" else 0
+            lift("EXK", o, w("FO", o, o + 128), 128, "FOk")
+            lift("EXK", o + 256, w("FO", o + 256, o + 384), 128, "FOq")
+            down(w(kq, o // 8, o // 8 + 8), "EXK", o, 128, "B1", "K%s%d" % (h, t))
+            down(w(kq, o // 8 + 8, o // 8 + 16), "EXK", o + 256, 128, "B1", "Q%s%d" % (h, t))
+
+        def firsts(h):
+            o, i = (16, 512) if h == "L" else (0, 0)
+            for b in range(4):
+                act(w("KB", i + 128 * b, i + 128 * b + 128), w("FH", 512 * b, 512 * b + 512).indirect(w(kq, o, o + 8)), AF.Copy, 1.0, ["FH%d" % b, "K%s%d" % (h, t)], ["KB%s%d" % (h, b)])
+
+        def second(h, b):
+            o, i = (24, 512) if h == "L" else (8, 0)
+            tt(w("A%s%d" % (h, t), b, 512, 4), w("FH", 512 * b, 512 * b + 512).indirect(w(kq, o, o + 8)), w("KB", i + 128 * b, i + 128 * b + 128), OP.add, ["FH%d" % b, "Q%s%d" % (h, t), "KB%s%d" % (h, b)], ["A%s%d.%d" % (h, t, b)])
+
+        def pack(h):
+            quant(w("A%sQ%d" % (h, t)), w("A%sS%d" % (h, t)), w("A%s%d" % (h, t)), ["A%s%d.%d" % (h, t, b) for b in range(4)], ["A%sQ%d" % (h, t)])
+
+        lists("K")
+        firsts("K")
+        cp(w("NMR"), w(lr).indirect(w(kq, 8, 16)), [lr, "QK%d" % t], ["NMR"])
+        second("K", 0)
+        lift("EXN", 0, w("NMR"), 128, "NMR")
+        second("K", 1)
+        down(w("NL%d" % t), "EXN", 0, 128, "B0", "NL%d" % t)
+        second("K", 2)
+        second("K", 3)
+        pack("K")
+        send(nxt, w("NLI%d" % t), w("NL%d" % t), "nma%d" % t, "nml%d" % t, ["NL%d" % t])
+        send(nxt, w("INQ%d" % t).bitcast(dt.uint8), w("AKQ%d" % t).bitcast(dt.uint8), "cda%d" % t, "cdl%d" % t, ["AKQ%d" % t], 2)
+        send(nxt, w("INS%d" % t), w("AKS%d" % t), "cda%d" % t, "cdl%d" % t, ["AKQ%d" % t], 2)
+        act(w("TR%d" % t), w(lr), AF.Copy, 1.0, [lr], ["TR%d" % t])
+        lists("L")
+        if last: turn_rows(t)
+        firsts("L")
+        if last: turn_send(t, prv)
+        for b in range(4): second("L", b)
+        pack("L")
+        lands(prv, "NLI%d" % t, "nma%d" % t)
+        lands(prv, "INQ%d" % t, "cda%d" % t, 2)
+
+        def layer(b, P, q, s, key, o, h):
+            mm(w(P, 0, 128), w("WQ", 128 * b, 128 * b + 128), w("WS", 128 * b, 128 * b + 128), w(q), w(s), True, True, ["WQ", "WS", key], [P])
+            act(w("HS", HW * b + o, HW * b + o + 128), w(P, 0, 128), AF.Copy, 0.03125, [P], ["HS%d%s" % (b, h)])
+
+        for b in range(4): layer(b, "P%d" % (0, 1, 6, 7)[b], "ALQ%d" % t, "ALS%d" % t, "ALQ%d" % t, 128, "L")
+        cp(w("EW").indirect(w(kq, 24, 32)), w("IOTA", 128, 256), ["QL%d" % t, "IOTA"], ["EW"])
+        cp(w("EW").indirect(w("NLI%d" % t)), w("IOTA", 0, 128), ["NLI%d" % t, "IOTA"], ["EW"])
+        lift("EXE", 0, w("EW"), 512, "EW")
+        down(w("EL"), "EXE", 0, 512, "B0", "EL")
+        for b in range(4): layer(b, "P%d" % (2 + b), "INQ%d" % t, "INS%d" % t, "INQ%d" % t, 0, "K")
+        for b in range(4):
+            tt(w("XN%d" % t, b, 2048, 4), w("HS", HW * b, HW * b + HW).indirect(w("EL")), w("FB", 512 * b, 512 * b + 512), OP.add, ["HS%dK" % b, "HS%dL" % b, "HSZ", "EL", "FB%d" % b], ["XN%d.%d" % (t, b)])
+        if not last: turn_rows(t)
+
+    t = ROUNDS - 1
+    lands(T.cores[(rank + 2 ** t) % N], "TRX%d" % t, "tra%d" % t)
+    dma("y", T["TRW%d" % t][0:128:16, :], w("TRX%d" % t), "trx%d" % t, 1, ["TRX%d" % t], ["TRW%d" % t])
+    stores, e = 13, 512 * ROUNDS
+    for h in range(2):
+        o = e + 256 * h
+        quant(w("XQ", o, o + 256), w("XS", o, o + 256), w("XN%d" % t, 1024 * h, 1024 * h + 1024), ["XN%d.%d" % (t, b) for b in range(4)], ["XQe%d" % h])
+        mm(w("P%d" % (6 + h), 0, 256), w("VQ"), w("VQS"), w("XQ", o, o + 256), w("XS", o, o + 256), True, True, ["VQ", "XQe%d" % h], ["P%d" % (6 + h)])
+    for h in range(2):
+        o = e + 256 * h
+        dma("y", T.oc[:, 1024 * h:1024 * h + 1024], w("XQ", o, o + 256).bitcast(dt.uint8), "st", stores, ["XQe%d" % h], ["oc%d" % h])
+    act(w("YS", 0, 256), w("P6", 0, 256), AF.Copy, 1.0, ["P6"], ["YSa"])
+    cp(w("YS", 256, 512), w("P7", 0, 256), ["P7"], ["YSb"])
+    dma("s", T.y[:, 0:256], w("YS", 0, 256), "st", stores, ["YSa"], ["ya"])
+    dma("y", T.y[:, 256:512], w("YS", 256, 512), "st", stores, ["YSb"], ["yb"])
+    for k in range(4):
+        for h in range(2):
+            o = e + 256 * h
+            dma("ys"[k % 2], T.osc[4 * k:4 * k + 4, 256 * h:256 * h + 256], T.XS[32 * k:32 * k + 4, o:o + 256], "st", stores, ["XQe%d" % h], ["osc%d%d" % (k, h)])
+    cp(w("OWS"), w("TRW%d" % t).indirect(w("LL%d" % t)), ["TRW%d" % t, "LL%d" % t], ["OWS"])
+    dma("y", T.lk[:, :], T.OWS[0:128:16, :], "st", stores, ["OWS"], ["lk"])
+    for sem in total:
+        if know["g"].get(sem, 0) < total[sem]: g.wait_ge(T.sem[sem], total[sem])

@@ -2,7 +2,7 @@ from concourse.mybir import dt, AluOpType as OP, ActivationFunctionType as AF
 
 N, ROUNDS = 4, 2
 HW = 264
-BIG = 2.0 ** 14
+BIG = 2.0 ** 16
 TC = [max(128, 64 * (k + 1)) for k in range(8)]
 TO = [sum(TC[:k]) for k in range(9)]
 CODES, F32, BF = "float8_e4m3fn_x4", "float32", "bfloat16"
@@ -15,7 +15,7 @@ def buf(names, cols, dtype, where="sbuf"):
 
 
 buf("X0 XN0 XN1 EB FH FB", 2048, BF)
-buf("UB VB ON OB BR0 BR1 TB0 TB1 AK0 AK1 AL0 AL1", 512, BF)
+buf("UB VB ON OB BS BR0 BR1 TB0 TB1 AK0 AK1 AL0 AL1", 512, BF)
 buf("UQ UR UT VQ OQ AKQ0 AKQ1 ALQ0 ALQ1 INQ0 INQ1", 128, CODES)
 buf("UQS URS UTS VQS OQS AKS0 AKS1 ALS0 ALS1 INS0 INS1", 128, "uint8")
 buf("WQ EQ", 512, CODES)
@@ -25,21 +25,22 @@ buf("XS", 512 * 3, "uint8")
 buf("QT", TO[8], CODES)
 buf("QS", TO[8], "uint8")
 buf("BT", 4 * TO[8], BF)
-buf("JUNK", 8448, BF)
+buf("JUNK", 7936, BF)
 buf("KB", 1024, BF)
 buf("LINKI", 32, "int32")
-buf("CA", 2560, F32)
-buf("CB", 2816, F32)
-buf("SM", 64, F32)
+buf("CA", 2608, F32)
+buf("CT", 560, F32)
+buf("CB", 1280, F32)
+buf("SM", 16, F32)
 buf("INT", 20, "int32")
 buf("UO", 16, "uint16")
-buf("W3", 1536, F32)
+buf("W3", 1568, F32)
 buf("RS", 32, F32)
-buf("WK", 128, F32)
-buf("EX", 2432, F32)
+buf("WK", 160, F32)
+buf("EX", 2944, F32)
 buf("II", 48, "int32")
 buf("U16", 80, "uint16")
-buf("OWS PAY POS POSA FO EW YS LR0 LR1 TR0 TR1 TRW0 TRW1", 512, F32)
+buf("OWS PAY POS POSA FO EW YS LKO LR0 LR1 TR0 TR1 TRW0 TRW1", 512, F32)
 buf("FF", 1024, F32)
 buf("NMR", 128, F32)
 buf("LQK0 LQK1", 256, F32)
@@ -51,18 +52,19 @@ buf("BRD0 BRD1 BRX0 BRX1", 32, BF, "dram")
 buf("P0 P1 P2 P3 P4 P5 P6 P7", 512, F32, "psum")
 
 PIECE = {
-    "AROW": ("CA", 0, 512), "M1": ("CA", 512, 512), "ML": ("CA", 1024, 512), "MX": ("CA", 1536, 512), "CR": ("CA", 2048, 512),
-    "IOTA": ("CB", 0, 512), "I4": ("CB", 512, 512), "CXA": ("CB", 1024, 512), "CXB": ("CB", 1536, 512), "CX": ("CB", 2048, 512), "ONEF": ("CB", 2560, 256),
-    "PM": ("SM", 0, 2), "PN": ("SM", 2, 2), "MC": ("SM", 4, 2), "B0": ("SM", 6, 1), "B1": ("SM", 7, 1), "R5": ("SM", 8, 32), "J16": ("SM", 40, 16),
+    "AROW": ("CA", 0, 512), "M1": ("CA", 512, 512), "MX": ("CA", 1024, 512), "CR": ("CA", 1536, 512), "CN": ("CA", 2048, 528),
+    "CX": ("CT", 0, 512), "R5": ("CT", 512, 32), "J16": ("CT", 544, 16),
+    "IOTA": ("CB", 0, 512), "I1": ("CB", 512, 512), "ONEF": ("CB", 1024, 256),
+    "PM": ("SM", 0, 2), "NPM": ("SM", 2, 1), "PMH": ("SM", 3, 1), "MC": ("SM", 4, 1),
     "UOI": ("INT", 0, 16), "PI": ("INT", 16, 2), "PJ": ("INT", 18, 2),
-    "MSK": ("W3", 0, 512), "SCN": ("W3", 512, 512), "SBD": ("W3", 1024, 512),
-    "RSI": ("WK", 0, 32), "RK": ("WK", 32, 32), "NX1": ("WK", 64, 16), "NX2": ("WK", 80, 16), "NN": ("WK", 96, 16), "TOT": ("WK", 112, 1),
-    "EXA": ("EX", 0, 512), "EXB": ("EX", 512, 256), "EXK": ("EX", 768, 512), "EXN": ("EX", 1280, 128), "EXE": ("EX", 1408, 512), "EXL": ("EX", 1920, 512),
+    "MSK": ("W3", 0, 528), "SCN": ("W3", 528, 528), "SBD": ("W3", 1056, 512),
+    "RSI": ("WK", 0, 32), "RK": ("WK", 32, 32), "NX1": ("WK", 64, 16), "NX2": ("WK", 80, 16), "NN": ("WK", 96, 16), "TOT": ("WK", 112, 1), "RSJ": ("WK", 128, 32),
+    "EXA": ("EX", 0, 512), "EXB": ("EX", 512, 256), "EXK": ("EX", 768, 512), "EXN": ("EX", 1280, 128), "EXE": ("EX", 1408, 512), "EXL": ("EX", 1920, 512), "DS": ("EX", 2432, 512),
     "CSL": ("II", 0, 32), "VL": ("II", 32, 16),
     "RKU": ("U16", 0, 32), "NU": ("U16", 32, 16), "EL": ("U16", 48, 32),
     "FR": ("FF", 0, 256), "F5": ("FF", 256, 256), "FC": ("FF", 512, 256), "VP": ("FF", 768, 256),
 }
-SEMAPHORES = ["cv", "cs", "ct", "cg", "ldx0", "ldx1", "ldu", "ldk", "ldv", "ldw", "st"]
+SEMAPHORES = ["cv", "cs", "ct", "cg", "ldx0", "ldx1", "ldu", "ldk", "ldv", "ldw", "ldc", "st"]
 for _t in range(ROUNDS):
     SEMAPHORES += [s + "%d" % _t for s in ("bro", "bra", "brl", "tbx", "nma", "nml", "cda", "cdl", "tro", "tra", "trl", "trx")]
 
@@ -144,15 +146,21 @@ def rank_program(g, core, T, topo):
     def cp(out, in_, reads, writes): op("v", lambda: V.tensor_copy(out, in_), reads, writes)
     def fill(out, c, writes): op("v", lambda: V.memset(out, c), [], writes)
     def act(out, in_, func, scale, reads, writes): op("s", lambda: S.activation(out, in_, func, scale=scale), reads, writes)
+    def actb(out, in_, func, bias, scale, reads, writes): op("s", lambda: S.activation(out, in_, func, bias=bias, scale=scale), reads, writes)
     def scan(out, d0, d1, reads, writes): op("v", lambda: V.tensor_tensor_scan(out, d0, d1, 0.0, OP.mult, OP.add), reads, writes)
     def quant(q, s, in_, reads, writes): op("v", lambda: V.quantize_mx(q, s, in_), reads, writes)
     def mm(out, a, asc, b, bsc, start, stop, reads, writes): op("t", lambda: g.tensor.matmul_mx(out, a, asc, b, bsc, start, stop), reads, writes)
+    def iota(out, pattern, base, cm, keys): op("g", lambda: G.iota(out, pattern, base, cm, allow_small_or_imprecise_dtypes=True), [], keys)
+    def iotai(out, pattern, base, cm, keys): op("g", lambda: G.iota(out, pattern, base, cm), [], keys)
+    def select(out, in_, pattern, cmp, c, base, cm, reads, writes): op("g", lambda: G.affine_select(out, in_, pattern, cmp, c, base, cm), reads, writes)
+
+    CXK = ["CT0"] + ["CX%d" % i for i in range(1, 8)]
 
     def lift(ex, a, row, n, key):
-        scan(w(ex, a, a + n), w("CX", 0, n), row, ["CX", key], ["%s.%d" % (ex, a)])
+        scan(w(ex, a, a + n), w("CX", 0, n), row, CXK + [key], ["%s.%d" % (ex, a)])
 
-    def down(out, ex, a, n, bias, key):
-        ts(out, w(ex, a + 15, a + n, 16), w("MC", 0, 1), w(bias), OP.mult, OP.add, ["%s.%d" % (ex, a), "MC", bias], [key])
+    def down(out, ex, a, n, less, key):
+        ts(out, w(ex, a + 15, a + n, 16), w("MC"), less, OP.mult, OP.add if less else None, ["%s.%d" % (ex, a), "MC"], [key])
 
     dma("s", w("UB"), T.u[:, :], "ldu", 1, [], ["UB"])
     dma("y", w("X0", 0, 1024), T.x[:, 0:1024], "ldx0", 1, [], ["X0a"])
@@ -162,59 +170,48 @@ def rank_program(g, core, T, topo):
     dma("y", w("WS"), T.ws[:, :], "ldw", 2, [], ["WS"])
     dma("y", w("VB"), T.v[:, :], "ldv", 1, [], ["VB"])
 
-    def iota(n, a, b, pattern, base, cm):
-        out = w(n, a, b)
-        if n in ("UOI", "PI"): op("g", lambda: G.iota(out, pattern, base, cm), [], [n])
-        else: op("g", lambda: G.iota(out, pattern, base, cm, allow_small_or_imprecise_dtypes=True), [], [n])
-
-    iota("UOI", 0, 16, [[1, 2], [16, 8]], 0, 0)
-    iota("PI", 0, 2, [[0, 2]], 0, 1)
-    iota("AROW", 0, 512, [[0, 32], [1, 16]], 0, 0)
-    fill(w("ON"), 1.0, ["ON"])
-    fill(w("EB"), 0.0, ["EB"])
+    iotai(w("PI"), [[0, 2]], 0, 1, ["PI"])
+    iota(w("AROW"), [[0, 32], [1, 16]], 0, 0, ["AROW"])
+    iotai(w("UOI"), [[1, 2], [16, 8]], 0, 0, ["UOI"])
     ts(w("PJ"), w("PI"), 15, None, OP.bitwise_and, None, ["PI"], ["PJ"])
-    cp(w("UO"), w("UOI"), ["UOI"], ["UO"])
+    fill(w("ON"), 1.0, ["ON"])
     cp(w("PM"), w("PJ"), ["PJ"], ["PM"])
     pm = w("PM", 0, 1)
-    ts(w("ML"), w("AROW"), pm, 2e25, OP.is_lt, OP.mult, ["AROW", "PM"], ["ML"])
-    ts(w("M1"), w("AROW"), pm, None, OP.is_equal, None, ["AROW", "PM"], ["M1"])
-    ts(w("CR"), w("AROW"), 0.0, None, OP.is_gt, None, ["AROW"], ["CR"])
-    op("s", lambda: S.activation(w("MX"), w("ML"), AF.Copy, bias=-1e25, scale=1.0), ["ML"], ["MX"])
-    for b in range(4):
-        op("g", lambda b=b: G.affine_select(w("EB", 512 * b + b, 512 * b + 512, 4), w("ON", 0, 128), [[-1, 128]], OP.is_equal, 0.0, 0, 1), ["ON", "EB"], ["EB%d" % b])
-    op("g", lambda: G.affine_select(w("OB"), w("ON"), [[-16, 8], [0, 64]], OP.is_ge, 0.0, 0, 1), ["ON"], ["OB"])
-    op("g", lambda: G.affine_select(w("OB"), w("OB"), [[16, 8], [0, 64]], OP.is_ge, 0.0, 15, -1), ["OB"], ["OB"])
-    iota("IOTA", 0, 512, [[1, 512]], 0, 0)
-    iota("I4", 0, 512, [[4, 512]], 4, 0)
-    iota("R5", 0, 32, [[-16, 32]], 511, 0)
-    iota("J16", 0, 16, [[16, 16]], 0, 0)
+    fill(w("MSK", 512, 528), 0.0, ["MSKp"])
+    fill(w("CN", 512, 528), 1.0, ["CNp"])
+    ts(w("NPM"), pm, -1.0, None, OP.mult, None, ["PM"], ["NPM"])
+    ts(w("PMH"), pm, 0.5, None, OP.subtract, None, ["PM"], ["PMH"])
+    for k in range(7, -1, -1):
+        fill(w("BT", 4 * TO[k] + 256 * k, 4 * TO[k + 1]), 0.0, ["BT%d.%d" % (k, s) for s in range(4)] + ["BT%dd" % k])
+    fill(w("RS", 0, 1), 0.0, ["RS0"])
+    cp(w("UO"), w("UOI"), ["UOI"], ["UO"])
+    actb(w("CN", 0, 512), w("AROW"), AF.Abs, w("NPM"), 1.0, ["AROW", "NPM"], ["CN"])
+    actb(w("M1"), w("CN", 0, 512), AF.Relu, 1.0, -1.0, ["CN"], ["M1"])
+    actb(w("MX"), w("AROW"), AF.Sign, w("PMH"), -1.0, ["AROW", "PMH"], ["MX"])
+    actb(w("CN", 0, 512), w("M1"), AF.Copy, 1.0, -1.0, ["M1"], ["CN"])
+    act(w("MX"), w("MX"), AF.Copy, 1e25, ["MX"], ["MX"])
+    act(w("CR"), w("AROW"), AF.Sign, 1.0, ["AROW"], ["CR"])
+    select(w("OB"), w("ON"), [[-16, 8], [0, 64]], OP.is_ge, 0.0, 0, 1, ["ON"], ["OB"])
+    select(w("OB"), w("OB"), [[16, 8], [0, 64]], OP.is_ge, 0.0, 15, -1, ["OB"], ["OB"])
+    for b in range(4): select(w("EB", 512 * b, 512 * b + 512), w("ON"), [[-4, 128], [-1, 4]], OP.is_equal, 0.0, b, 4, ["ON"], ["EB%d" % b])
+    iota(w("IOTA"), [[1, 512]], 0, 0, ["IOTA"])
     quant(w("UQ"), w("UQS"), w("UB"), ["UB"], ["UQ"])
-    for k in range(8):
-        fill(w("BT", 4 * TO[k] + 256 * k, 4 * TO[k + 1]), 0.0, ["BT%d.%d%s" % (k, s, h) for s in range(4) for h in "ad"])
-    for q, o in (("UR", 0), ("UT", 8)):
+
+    def pick_u(q, o):
         cp(w(q).bitcast(dt.uint32), w("UQ").bitcast(dt.uint32).indirect(w("UO", o, o + 8)), ["UQ", "UO"], [q])
         cp(w(q + "S"), w("UQS").indirect(w("UO", o, o + 8)), ["UQ", "UO"], [q + "S"])
 
-    def late_constants():
-        quant(w("EQ"), w("EQS"), w("EB"), ["EB%d" % b for b in range(4)] + ["EB"], ["EQ"])
-        quant(w("OQ"), w("OQS"), w("OB"), ["OB"], ["OQ"])
-        cp(w("LL0"), w("LINKI"), ["LINKI"], ["LL0"])
-        ts(w("PN"), w("PM"), 1.0, None, OP.add, None, ["PM"], ["PN"])
-
     def later_constants():
-        ts(w("CXA"), w("AROW"), pm, None, OP.is_gt, None, ["AROW", "PM"], ["CXA"])
-        ts(w("CXB"), w("AROW"), w("PN", 0, 1), BIG - 1.0, OP.is_equal, OP.mult, ["AROW", "PN"], ["CXB"])
-        ts(w("MC"), w("PM"), 15.0, 1.0 - 1.0 / BIG, OP.is_equal, OP.mult, ["PM"], ["MC"])
-        tt(w("CX"), w("CXA"), w("CXB"), OP.add, ["CXA", "CXB"], ["CX"])
-        ts(w("B0"), pm, 15.0, -0.468, OP.is_lt, OP.mult, ["PM"], ["B0"])
-        ts(w("R5"), w("R5"), pm, None, OP.subtract, None, ["R5", "PM"], ["R5"])
-        ts(w("MC"), w("MC"), 1.0 / BIG, None, OP.add, None, ["MC"], ["MC"])
-        ts(w("B1"), w("B0"), 1.0, None, OP.subtract, None, ["B0"], ["B1"])
-        ts(w("J16"), w("J16"), pm, None, OP.add, None, ["J16", "PM"], ["J16"])
-        fill(w("ONEF"), 1.0, ["ONEF"])
-        fill(w("HS"), 0.0, ["HS%d%s" % (b, h) for b in range(4) for h in "KL"] + ["HSZ"])
-        quant(w("VQ"), w("VQS"), w("VB"), ["VB"], ["VQ"])
-        fill(w("TRW1"), 0.0, ["TRW1"])
+        iota(T.CT[0:16, 0:512], [[0, 512]], 1, 0, ["CTx"])
+        select(T.CT[0:16, 0:512], T.CT[0:16, 0:512], [[0, 32], [1, 16]], OP.is_gt, 0.0, 0, -1, ["CTx"], ["CTx"])
+        select(T.CT[0:16, 0:512], T.CT[0:16, 0:512], [[0, 32], [1, 16]], OP.not_equal, BIG, -1, -1, ["CTx"], ["CTx"])
+        iota(T.CT[0:16, 512:544], [[-16, 32]], 511, -1, ["CTy"])
+        iota(T.CT[0:16, 544:560], [[16, 16]], 0, 1, ["CTz", "CT0"])
+        for i in range(1, 8): dma("y", T.CT[16 * i:16 * i + 16, :], T.CT[0:16, :], "ldc", 7, ["CTx", "CTy", "CTz"], ["CX%d" % i])
+        iota(w("I1"), [[1, 512]], 1, 0, ["I1"])
+        iota(w("ONEF"), [[0, 256]], 1, 0, ["ONEF"])
+        for b in range(4): iota(w("HS", HW * b + 256, HW * b + HW), [[0, 8]], 0, 0, ["HSZ%d" % b])
+        iota(w("TRW1"), [[0, 512]], 0, 0, ["TRW1"])
 
     def turn_rows(t):
         n, lr = "LQK%d" % t, "LR%d" % t
@@ -227,7 +224,7 @@ def rank_program(g, core, T, topo):
         dma("y", w("TRD%d" % t), T[tr][0:128:16, :], "tro%d" % t, 1, [tr], ["TRD%d" % t])
         send(back, w("TRX%d" % t), w("TRD%d" % t), "tra%d" % t, "trl%d" % t, ["TRD%d" % t])
 
-    def spread(n, src, key, sem):
+    def spread(n, src, sem):
         for a in range(16): dma("y", T[n][a:128:16, :], w(src), sem, 16, [src], ["%s.%d" % (n, a)])
 
     for t in range(ROUNDS):
@@ -238,29 +235,31 @@ def rank_program(g, core, T, topo):
         xq, xs = w("XQ", 512 * t, 512 * t + 512), w("XS", 512 * t, 512 * t + 512)
         kx = "XQ%d" % t
         ll, lr, kq, br, tb = ("%s%d" % (n, t) for n in ("LL", "LR", "KQ", "BR", "TB"))
+        if t == 0: pick_u("UR", 0)
         quant(xq, xs, w(X), xk, [kx])
+        if t == 0: pick_u("UT", 8)
         mm(w("P0"), w("UR"), w("URS"), xq, xs, True, True, ["UR", "URS", kx], ["P0"])
         mm(w("P1"), w("UT"), w("UTS"), xq, xs, True, True, ["UT", "UTS", kx], ["P1"])
         if t: turn_send(t - 1, T.cores[(rank - d // 2) % N])
-        tt(w("MSK"), w("P0"), w("M1"), OP.mult, ["P0", "M1"], ["MSK"])
-        ts(w(br), w("P1"), 0.0, 0.5, OP.is_gt, OP.subtract, ["P1"], [br])
-        scan(w("SCN"), w("CR"), w("MSK"), ["CR", "MSK"], ["SCN"])
+        act(w("BS"), w("P1"), AF.Sign, 1.0, ["P1"], ["BS"])
+        actb(w(br), w("BS"), AF.Sign, -0.5, 1.0, ["BS"], [br])
+        tt(w("MSK", 0, 512), w("P0"), w("M1"), OP.mult, ["P0", "M1"], ["MSK"])
         tt(w("SBD"), w("P0"), w("MX"), OP.min, ["P0", "MX"], ["SBD"])
+        scan(w("SCN"), w("CN"), w("MSK"), ["CN", "CNp", "MSK", "MSKp"], ["SCN"])
         dma("y", w("BRD%d" % t), T[br][0:128:16, :], "bro%d" % t, 1, [br], ["BRD%d" % t])
         send(prv, w("BRX%d" % t), w("BRD%d" % t), "bra%d" % t, "brl%d" % t, ["BRD%d" % t])
         if t:
             p = t - 1
             lands(T.cores[(rank + d // 2) % N], "TRX%d" % p, "tra%d" % p)
-            spread("TRW%d" % p, "TRX%d" % p, "", "trx%d" % p)
+            spread("TRW%d" % p, "TRX%d" % p, "trx%d" % p)
         lands(nxt, "BRX%d" % t, "bra%d" % t)
-        spread(tb, "BRX%d" % t, "", "tbx%d" % t)
-        if t == 0: late_constants()
-        for b in range(4):
-            mm(w("P%d" % (2 + b)), w("EQ", 128 * b, 128 * b + 128), w("EQS", 128 * b, 128 * b + 128), xq, xs, True, True, ["EQ", kx], ["P%d" % (2 + b)])
+        spread(tb, "BRX%d" % t, "tbx%d" % t)
+        if t == 0: later_constants()
+        iota(w("EW"), [[0, 512]], 256, 0, ["EW"])
 
         def colsum(k):
             q, s = w("QT", TO[k], TO[k + 1]), w("QS", TO[k], TO[k + 1])
-            quant(q, s, w("BT", 4 * TO[k], 4 * TO[k + 1]), ["BT%d.%d%s" % (k, i, h) for i in range(4) for h in "ad"], ["QT%d" % k])
+            quant(q, s, w("BT", 4 * TO[k], 4 * TO[k + 1]), ["BT%d.%d" % (k, i) for i in range(4)] + ["BT%dd" % k], ["QT%d" % k])
             mm(w("P6", 0, TC[k]), w("OQ"), w("OQS"), q, s, k == 7, k == 0, ["OQ", "QT%d" % k], ["P6"])
 
         for k in range(7, -1, -1):
@@ -269,24 +268,40 @@ def rank_program(g, core, T, topo):
                 c = 4 * k + i
                 key = "BT%d.%d" % (k, i)
                 sc = w("SCN", 16 * c + 15, 16 * c + 16)
-                if c: ts(w("BT", o + i, o + 64 * c, 4), w("P0", 0, 16 * c), sc, None, OP.is_ge, None, ["P0", "SCN"], [key + "a"])
-                ts(w("BT", o + 64 * c + i, o + 64 * c + 64, 4), w("SBD", 16 * c, 16 * c + 16), sc, None, OP.is_ge, None, ["SBD", "SCN"], [key + "d"])
-                j = 8 * c * (c + 1)
-                op("s", lambda: S.activation(w("JUNK", j, j + 16 * c + 16), w("BT", o + i, o + 64 * c + 64, 4), AF.Copy, accum_out=w("RS", c, c + 1)), [key + "a", key + "d"], ["JUNK%d" % c, "RS%d" % c])
-                if i == 3 and k < 7: colsum(k + 1)
-            if k == 6:
-                if t == 0: later_constants()
-                tt(w("OWS"), w(br), w("I4"), OP.mult, [br, "I4"], ["OWS"])
-            if k == 5 and t == 0: act(w(lr), w("IOTA").indirect(w(ll)), AF.Copy, 1.0, ["IOTA", ll], [lr])
-            if k == 3 and t: act(w(lr), w("TRW%d" % (t - 1)).indirect(w("LL%d" % (t - 1))), AF.Copy, 1.0, ["TRW%d.%d" % (t - 1, a) for a in range(16)] + ["LL%d" % (t - 1)], [lr])
+                if c:
+                    ts(w("BT", o + i, o + 64 * c, 4), w("P0", 0, 16 * c), sc, None, OP.is_ge, None, ["P0", "SCN"], [key])
+                    j = 8 * c * (c - 1)
+                    op("s", lambda: S.activation(w("JUNK", j, j + 16 * c), w("BT", o + i, o + 64 * c, 4), AF.Copy, accum_out=w("RS", c, c + 1)), [key], ["JUNK%d" % c, "RS%d" % c])
+                if i == 3:
+                    tt(w("BT", o + 256 * k, o + 256 * k + 256, 4), w("SBD", 64 * k, 64 * k + 64), w("SCN", 64 * k + 16, 64 * k + 80), OP.is_ge, ["SBD", "SCN"], ["BT%dd" % k])
+                    if k < 7: colsum(k + 1)
+                if i == 1: scan(w("DS", 64 * k, 64 * k + 64), w("CR", 64 * k, 64 * k + 64), w("BT", o + 256 * k, o + 256 * k + 256, 4), ["CR", "BT%dd" % k], ["DS%d" % k])
+            if k == 7 and t == 0:
+                quant(w("OQ"), w("OQS"), w("OB"), ["OB"], ["OQ"])
+                cp(w("LL0"), w("LINKI"), ["LINKI"], ["LL0"])
+            if k == 6 and t == 0:
+                quant(w("EQ"), w("EQS"), w("EB"), ["EB%d" % b for b in range(4)], ["EQ"])
+                ts(w("MC"), pm, 15.0, 1.0 - 1.0 / BIG, OP.is_equal, OP.mult, ["PM"], ["MC"])
+            if k == 7 and t or k == 6 and not t:
+                for b in range(4):
+                    mm(w("P%d" % (2 + b)), w("EQ", 128 * b, 128 * b + 128), w("EQS", 128 * b, 128 * b + 128), xq, xs, True, True, ["EQ", kx], ["P%d" % (2 + b)])
+            if k == 5:
+                if t == 0: ts(w("MC"), w("MC"), 1.0 / BIG, None, OP.add, None, ["MC"], ["MC"])
+                if t == 0: act(w(lr), w("IOTA").indirect(w(ll)), AF.Copy, 1.0, ["IOTA", ll], [lr])
+            if k == 3:
+                if t: act(w(lr), w("TRW%d" % (t - 1)).indirect(w("LL%d" % (t - 1))), AF.Copy, 1.0, ["TRW%d.%d" % (t - 1, a) for a in range(16)] + ["LL%d" % (t - 1)], [lr])
+                tt(w("OWS"), w(br), w("I1"), OP.mult, [br, "I1"], ["OWS"])
             if k == 1 and t: lift("EXL", 0, w(lr), 512, lr)
-        if t: down(w(ll), "EXL", 0, 512, "B0", ll)
+        if t: down(w(ll), "EXL", 0, 512, None, ll)
+        else: quant(w("VQ"), w("VQS"), w("VB"), ["VB"], ["VQ"])
         colsum(0)
         for b in range(4): act(w("FH", 512 * b, 512 * b + 512), w("P%d" % (2 + b)), AF.Copy, 0.5, ["P%d" % (2 + b)], ["FH%d" % b])
+        act(w("TR%d" % t), w(lr), AF.Copy, 1.0, [lr], ["TR%d" % t])
+        tt(w("RSJ"), w("DS", 15, 512, 16), w("R5"), OP.add, ["DS%d" % c for c in range(8)] + CXK, ["RSJ"])
         tt(w("PAY"), w(tb).indirect(w(ll)), w("OWS"), OP.mult, ["%s.%d" % (tb, a) for a in range(16)] + [ll, "OWS"], ["PAY"])
-        tt(w("RSI"), w("RS"), w("R5"), OP.add, ["RS%d" % c for c in range(32)] + ["R5"], ["RSI"])
         lift("EXA", 0, w("P6"), 512, "P6")
-        down(w("CSL"), "EXA", 0, 512, "B0", "CSL")
+        tt(w("RSI"), w("RS"), w("RSJ"), OP.add, ["RS%d" % c for c in range(32)] + ["RSJ"], ["RSI"])
+        down(w("CSL"), "EXA", 0, 512, None, "CSL")
         tt(w("RK"), w("RSI"), w("CSL"), OP.subtract, ["RSI", "CSL"], ["RK"])
         cp(w("RKU"), w("RK"), ["RK"], ["RKU"])
         cp(w("POS").indirect(w("RKU")), w("PAY"), ["RKU", "PAY"], ["POS"])
@@ -294,12 +309,11 @@ def rank_program(g, core, T, topo):
         ts(w("FR"), w("POS", 1, 512, 2), 0.0, None, OP.is_lt, None, ["POS"], ["FR"])
         ts(w("F5"), w("POS", 1, 512, 2), 0.0, 512.0, OP.is_lt, OP.mult, ["POS"], ["F5"])
         scan(w("FC"), w("ONEF"), w("FR"), ["ONEF", "FR"], ["FC"])
-        fill(w("EW"), 256.0, ["EW"])
         tt(w("VP"), w("FC"), w("F5"), OP.add, ["FC", "F5"], ["VP"])
         ts(w("TOT"), w("FC", 255, 256), -1.0, -257.0, OP.mult, OP.add, ["FC"], ["TOT"])
         lift("EXB", 0, w("VP"), 256, "VP")
-        down(w("VL"), "EXB", 0, 256, "B0", "VL")
-        tt(w("NX1"), w("J16"), w("VL"), OP.subtract, ["J16", "VL"], ["NX1"])
+        down(w("VL"), "EXB", 0, 256, None, "VL")
+        tt(w("NX1"), w("J16"), w("VL"), OP.subtract, CXK + ["VL"], ["NX1"])
         ts(w("NX2"), w("VL"), w("TOT"), None, OP.add, None, ["VL", "TOT"], ["NX2"])
         tt(w("NN"), w("NX1"), w("NX2"), OP.max, ["NX1", "NX2"], ["NN"])
         cp(w("NU"), w("NN"), ["NN"], ["NU"])
@@ -311,8 +325,8 @@ def rank_program(g, core, T, topo):
             o = 128 if h == "L" else 0
             lift("EXK", o, w("FO", o, o + 128), 128, "FOk")
             lift("EXK", o + 256, w("FO", o + 256, o + 384), 128, "FOq")
-            down(w(kq, o // 8, o // 8 + 8), "EXK", o, 128, "B1", "K%s%d" % (h, t))
-            down(w(kq, o // 8 + 8, o // 8 + 16), "EXK", o + 256, 128, "B1", "Q%s%d" % (h, t))
+            down(w(kq, o // 8, o // 8 + 8), "EXK", o, 128, -1.0, "K%s%d" % (h, t))
+            down(w(kq, o // 8 + 8, o // 8 + 16), "EXK", o + 256, 128, -1.0, "Q%s%d" % (h, t))
 
         def firsts(h):
             o, i = (16, 512) if h == "L" else (0, 0)
@@ -332,14 +346,13 @@ def rank_program(g, core, T, topo):
         second("K", 0)
         lift("EXN", 0, w("NMR"), 128, "NMR")
         second("K", 1)
-        down(w("NL%d" % t), "EXN", 0, 128, "B0", "NL%d" % t)
+        down(w("NL%d" % t), "EXN", 0, 128, None, "NL%d" % t)
         second("K", 2)
         second("K", 3)
         pack("K")
         send(nxt, w("NLI%d" % t), w("NL%d" % t), "nma%d" % t, "nml%d" % t, ["NL%d" % t])
         send(nxt, w("INQ%d" % t).bitcast(dt.uint8), w("AKQ%d" % t).bitcast(dt.uint8), "cda%d" % t, "cdl%d" % t, ["AKQ%d" % t], 2)
         send(nxt, w("INS%d" % t), w("AKS%d" % t), "cda%d" % t, "cdl%d" % t, ["AKQ%d" % t], 2)
-        act(w("TR%d" % t), w(lr), AF.Copy, 1.0, [lr], ["TR%d" % t])
         lists("L")
         if last: turn_rows(t)
         firsts("L")
@@ -357,10 +370,10 @@ def rank_program(g, core, T, topo):
         cp(w("EW").indirect(w(kq, 24, 32)), w("IOTA", 128, 256), ["QL%d" % t, "IOTA"], ["EW"])
         cp(w("EW").indirect(w("NLI%d" % t)), w("IOTA", 0, 128), ["NLI%d" % t, "IOTA"], ["EW"])
         lift("EXE", 0, w("EW"), 512, "EW")
-        down(w("EL"), "EXE", 0, 512, "B0", "EL")
+        down(w("EL"), "EXE", 0, 512, None, "EL")
         for b in range(4): layer(b, "P%d" % (2 + b), "INQ%d" % t, "INS%d" % t, "INQ%d" % t, 0, "K")
         for b in range(4):
-            tt(w("XN%d" % t, b, 2048, 4), w("HS", HW * b, HW * b + HW).indirect(w("EL")), w("FB", 512 * b, 512 * b + 512), OP.add, ["HS%dK" % b, "HS%dL" % b, "HSZ", "EL", "FB%d" % b], ["XN%d.%d" % (t, b)])
+            tt(w("XN%d" % t, b, 2048, 4), w("HS", HW * b, HW * b + HW).indirect(w("EL")), w("FB", 512 * b, 512 * b + 512), OP.add, ["HS%dK" % b, "HS%dL" % b, "HSZ%d" % b, "EL", "FB%d" % b], ["XN%d.%d" % (t, b)])
         if not last: turn_rows(t)
 
     t = ROUNDS - 1
@@ -371,18 +384,16 @@ def rank_program(g, core, T, topo):
         o = e + 256 * h
         quant(w("XQ", o, o + 256), w("XS", o, o + 256), w("XN%d" % t, 1024 * h, 1024 * h + 1024), ["XN%d.%d" % (t, b) for b in range(4)], ["XQe%d" % h])
         mm(w("P%d" % (6 + h), 0, 256), w("VQ"), w("VQS"), w("XQ", o, o + 256), w("XS", o, o + 256), True, True, ["VQ", "XQe%d" % h], ["P%d" % (6 + h)])
-    for h in range(2):
-        o = e + 256 * h
         dma("y", T.oc[:, 1024 * h:1024 * h + 1024], w("XQ", o, o + 256).bitcast(dt.uint8), "st", stores, ["XQe%d" % h], ["oc%d" % h])
     act(w("YS", 0, 256), w("P6", 0, 256), AF.Copy, 1.0, ["P6"], ["YSa"])
     cp(w("YS", 256, 512), w("P7", 0, 256), ["P7"], ["YSb"])
     dma("s", T.y[:, 0:256], w("YS", 0, 256), "st", stores, ["YSa"], ["ya"])
     dma("y", T.y[:, 256:512], w("YS", 256, 512), "st", stores, ["YSb"], ["yb"])
+    act(w("LKO"), w("TRW%d" % t).indirect(w("LL%d" % t)), AF.Copy, 1.0, ["TRW%d" % t, "LL%d" % t], ["LKO"])
+    dma("s", T.lk[:, :], T.LKO[0:128:16, :], "st", stores, ["LKO"], ["lk"])
     for k in range(4):
         for h in range(2):
             o = e + 256 * h
-            dma("ys"[k % 2], T.osc[4 * k:4 * k + 4, 256 * h:256 * h + 256], T.XS[32 * k:32 * k + 4, o:o + 256], "st", stores, ["XQe%d" % h], ["osc%d%d" % (k, h)])
-    cp(w("OWS"), w("TRW%d" % t).indirect(w("LL%d" % t)), ["TRW%d" % t, "LL%d" % t], ["OWS"])
-    dma("y", T.lk[:, :], T.OWS[0:128:16, :], "st", stores, ["OWS"], ["lk"])
+            dma("y", T.osc[4 * k:4 * k + 4, 256 * h:256 * h + 256], T.XS[32 * k:32 * k + 4, o:o + 256], "st", stores, ["XQe%d" % h], ["osc%d%d" % (k, h)])
     for sem in total:
         if know["g"].get(sem, 0) < total[sem]: g.wait_ge(T.sem[sem], total[sem])

from concourse.mybir import dt, AluOpType as OP, ActivationFunctionType as AF

N, ROUNDS = 4, 2
HW = 264
BIG = 2.0 ** 16
TC = [max(128, 64 * (k + 1)) for k in range(8)]
TO = [sum(TC[:k]) for k in range(9)]
CODES, F32, BF = "float8_e4m3fn_x4", "float32", "bfloat16"

SCRATCH = {}


def buf(names, cols, dtype, where="sbuf"):
    for n in names.split(): SCRATCH[n] = (where, [128, cols], dtype)


buf("X0 XN0 XN1 EB FH FB", 2048, BF)
buf("UB VB ON OB BS BR0 BR1 TB0 TB1 AK0 AK1 AL0 AL1", 512, BF)
buf("UQ UR UT VQ OQ AKQ0 AKQ1 ALQ0 ALQ1 INQ0 INQ1", 128, CODES)
buf("UQS URS UTS VQS OQS AKS0 AKS1 ALS0 ALS1 INS0 INS1", 128, "uint8")
buf("WQ EQ", 512, CODES)
buf("WS EQS", 512, "uint8")
buf("XQ", 512 * 3, CODES)
buf("XS", 512 * 3, "uint8")
buf("QT", TO[8], CODES)
buf("QS", TO[8], "uint8")
buf("BT", 4 * TO[8], BF)
buf("JUNK", 7936, BF)
buf("KB", 1024, BF)
buf("LINKI", 32, "int32")
buf("CA", 2608, F32)
buf("CT", 560, F32)
buf("CB", 1280, F32)
buf("SM", 16, F32)
buf("INT", 20, "int32")
buf("UO", 16, "uint16")
buf("W3", 1568, F32)
buf("RS", 32, F32)
buf("WK", 160, F32)
buf("EX", 2944, F32)
buf("II", 48, "int32")
buf("U16", 80, "uint16")
buf("OWS PAY POS POSA FO EW YS LKO LR0 LR1 TR0 TR1 TRW0 TRW1", 512, F32)
buf("FF", 1024, F32)
buf("NMR", 128, F32)
buf("LQK0 LQK1", 256, F32)
buf("HS", 4 * HW, F32)
buf("KQ0 KQ1 LL0 LL1", 32, "uint16")
buf("NL0 NL1 NLI0 NLI1", 8, "uint16")
buf("TRD0 TRD1 TRX0 TRX1", 32, F32, "dram")
buf("BRD0 BRD1 BRX0 BRX1", 32, BF, "dram")
buf("P0 P1 P2 P3 P4 P5 P6 P7", 512, F32, "psum")

PIECE = {
    "AROW": ("CA", 0, 512), "M1": ("CA", 512, 512), "MX": ("CA", 1024, 512), "CR": ("CA", 1536, 512), "CN": ("CA", 2048, 528),
    "CX": ("CT", 0, 512), "R5": ("CT", 512, 32), "J16": ("CT", 544, 16),
    "IOTA": ("CB", 0, 512), "I1": ("CB", 512, 512), "ONEF": ("CB", 1024, 256),
    "PM": ("SM", 0, 2), "NPM": ("SM", 2, 1), "PMH": ("SM", 3, 1), "MC": ("SM", 4, 1),
    "UOI": ("INT", 0, 16), "PI": ("INT", 16, 2), "PJ": ("INT", 18, 2),
    "MSK": ("W3", 0, 528), "SCN": ("W3", 528, 528), "SBD": ("W3", 1056, 512),
    "RSI": ("WK", 0, 32), "RK": ("WK", 32, 32), "NX1": ("WK", 64, 16), "NX2": ("WK", 80, 16), "NN": ("WK", 96, 16), "TOT": ("WK", 112, 1), "RSJ": ("WK", 128, 32),
    "EXA": ("EX", 0, 512), "EXB": ("EX", 512, 256), "EXK": ("EX", 768, 512), "EXN": ("EX", 1280, 128), "EXE": ("EX", 1408, 512), "EXL": ("EX", 1920, 512), "DS": ("EX", 2432, 512),
    "CSL": ("II", 0, 32), "VL": ("II", 32, 16),
    "RKU": ("U16", 0, 32), "NU": ("U16", 32, 16), "EL": ("U16", 48, 32),
    "FR": ("FF", 0, 256), "F5": ("FF", 256, 256), "FC": ("FF", 512, 256), "VP": ("FF", 768, 256),
}
SEMAPHORES = ["cv", "cs", "ct", "cg", "ldx0", "ldx1", "ldu", "ldk", "ldv", "ldw", "ldc", "st"]
for _t in range(ROUNDS):
    SEMAPHORES += [s + "%d" % _t for s in ("bro", "bra", "brl", "tbx", "nma", "nml", "cda", "cdl", "tro", "tra", "trl", "trx")]


def rank_program(g, core, T, topo):
    rank = T.rank_of(core)
    if rank is None:
        return
    queue = {"v": g.vector, "s": g.scalar, "t": g.tensor, "g": g, "y": g.sync}
    own = {"v": "cv", "s": "cs", "t": "ct", "g": "cg"}
    count = {"cv": 0, "cs": 0, "ct": 0, "cg": 0}
    total = {}
    know = {q: {} for q in queue}
    wrote, read = {}, {}

    def w(n, a=0, b=None, step=1):
        if n in PIECE: name, off, width = PIECE[n]
        else: name, off, width = n, 0, SCRATCH[n][1][1]
        if b is None: b = width
        if step == 1: return T[name][:, off + a:off + b]
        return T[name][:, off + a:off + b:step]

    def settle(q, reads, writes):
        need = []
        for k in reads:
            if k in wrote: need.append(wrote[k])
            if k[0] == "P" and k[1:].isdigit():
                need += [r for r in read.get(k, []) if r[0] != q]
        for k in writes:
            if k in wrote: need.append(wrote[k])
            need += [r for r in read.get(k, []) if r[0] != q or r[1] not in count]
        need.sort(key=lambda n: -n[2])
        for _, sem, val, seen in need:
            if know[q].get(sem, 0) >= val: continue
            queue[q].wait_ge(T.sem[sem], val)
            know[q][sem] = val
            for s2 in seen: know[q][s2] = max(know[q].get(s2, 0), seen[s2])

    def note(token, reads, writes):
        for k in reads: read.setdefault(k, []).append(token)
        for k in writes:
            wrote[k] = token
            read[k] = []

    def op(q, call, reads, writes):
        settle(q, reads, writes)
        sem = own[q]
        call().then_inc(T.sem[sem], 1)
        count[sem] += 1
        total[sem] = count[sem]
        note((q, sem, count[sem], dict(know[q])), reads, writes)

    def dma(q, out, in_, sem, of, reads, writes):
        settle(q, reads, writes)
        queue[q].dma_start(out, in_).then_inc(T.sem[sem], 16)
        total[sem] = 16 * of
        note((q, sem, 16 * of, dict(know[q])), reads, writes)

    def send(dst, out, in_, rsem, lsem, reads, of=1):
        settle("g", reads, [])
        rid, pid = topo.addr(dst)[:2]
        n = len(topo.engines(core, dst))
        g.remote_dma(out, in_, T.sem[rsem], T.sem[lsem], pid, rid, topo.mask(core, dst))
        total[lsem] = n * of
        note(("g", lsem, n * of, dict(know["g"])), reads, [])

    def lands(src, key, rsem, of=1):
        n = len(topo.engines(src, core)) * of
        total[rsem] = n
        note(("far", rsem, n, {}), [], [key])

    V, S, G = g.vector, g.scalar, g

    def ts(out, in0, a, b, op0, op1, reads, writes):
        if op1 is None: op("v", lambda: V.tensor_scalar(out, in0, a, None, op0), reads, writes)
        else: op("v", lambda: V.tensor_scalar(out, in0, a, b, op0, op1), reads, writes)

    def tt(out, in0, in1, o, reads, writes): op("v", lambda: V.tensor_tensor(out, in0, in1, o), reads, writes)
    def cp(out, in_, reads, writes): op("v", lambda: V.tensor_copy(out, in_), reads, writes)
    def fill(out, c, writes): op("v", lambda: V.memset(out, c), [], writes)
    def act(out, in_, func, scale, reads, writes): op("s", lambda: S.activation(out, in_, func, scale=scale), reads, writes)
    def actb(out, in_, func, bias, scale, reads, writes): op("s", lambda: S.activation(out, in_, func, bias=bias, scale=scale), reads, writes)
    def scan(out, d0, d1, reads, writes): op("v", lambda: V.tensor_tensor_scan(out, d0, d1, 0.0, OP.mult, OP.add), reads, writes)
    def quant(q, s, in_, reads, writes): op("v", lambda: V.quantize_mx(q, s, in_), reads, writes)
    def mm(out, a, asc, b, bsc, start, stop, reads, writes): op("t", lambda: g.tensor.matmul_mx(out, a, asc, b, bsc, start, stop), reads, writes)
    def iota(out, pattern, base, cm, keys): op("g", lambda: G.iota(out, pattern, base, cm, allow_small_or_imprecise_dtypes=True), [], keys)
    def iotai(out, pattern, base, cm, keys): op("g", lambda: G.iota(out, pattern, base, cm), [], keys)
    def select(out, in_, pattern, cmp, c, base, cm, reads, writes): op("g", lambda: G.affine_select(out, in_, pattern, cmp, c, base, cm), reads, writes)

    CXK = ["CT0"] + ["CX%d" % i for i in range(1, 8)]

    def lift(ex, a, row, n, key):
        scan(w(ex, a, a + n), w("CX", 0, n), row, CXK + [key], ["%s.%d" % (ex, a)])

    def down(out, ex, a, n, less, key):
        ts(out, w(ex, a + 15, a + n, 16), w("MC"), less, OP.mult, OP.add if less else None, ["%s.%d" % (ex, a), "MC"], [key])

    dma("s", w("UB"), T.u[:, :], "ldu", 1, [], ["UB"])
    dma("y", w("X0", 0, 1024), T.x[:, 0:1024], "ldx0", 1, [], ["X0a"])
    dma("s", w("X0", 1024, 2048), T.x[:, 1024:2048], "ldx1", 1, [], ["X0b"])
    dma("y", w("LINKI"), T.link[:, :], "ldk", 1, [], ["LINKI"])
    dma("y", w("WQ").bitcast(dt.uint8), T.wc[:, :], "ldw", 2, [], ["WQ"])
    dma("y", w("WS"), T.ws[:, :], "ldw", 2, [], ["WS"])
    dma("y", w("VB"), T.v[:, :], "ldv", 1, [], ["VB"])

    iotai(w("PI"), [[0, 2]], 0, 1, ["PI"])
    iota(w("AROW"), [[0, 32], [1, 16]], 0, 0, ["AROW"])
    iotai(w("UOI"), [[1, 2], [16, 8]], 0, 0, ["UOI"])
    ts(w("PJ"), w("PI"), 15, None, OP.bitwise_and, None, ["PI"], ["PJ"])
    fill(w("ON"), 1.0, ["ON"])
    cp(w("PM"), w("PJ"), ["PJ"], ["PM"])
    pm = w("PM", 0, 1)
    fill(w("MSK", 512, 528), 0.0, ["MSKp"])
    fill(w("CN", 512, 528), 1.0, ["CNp"])
    ts(w("NPM"), pm, -1.0, None, OP.mult, None, ["PM"], ["NPM"])
    ts(w("PMH"), pm, 0.5, None, OP.subtract, None, ["PM"], ["PMH"])
    for k in range(7, -1, -1):
        fill(w("BT", 4 * TO[k] + 256 * k, 4 * TO[k + 1]), 0.0, ["BT%d.%d" % (k, s) for s in range(4)] + ["BT%dd" % k])
    fill(w("RS", 0, 1), 0.0, ["RS0"])
    cp(w("UO"), w("UOI"), ["UOI"], ["UO"])
    actb(w("CN", 0, 512), w("AROW"), AF.Abs, w("NPM"), 1.0, ["AROW", "NPM"], ["CN"])
    actb(w("M1"), w("CN", 0, 512), AF.Relu, 1.0, -1.0, ["CN"], ["M1"])
    actb(w("MX"), w("AROW"), AF.Sign, w("PMH"), -1.0, ["AROW", "PMH"], ["MX"])
    actb(w("CN", 0, 512), w("M1"), AF.Copy, 1.0, -1.0, ["M1"], ["CN"])
    act(w("MX"), w("MX"), AF.Copy, 1e25, ["MX"], ["MX"])
    act(w("CR"), w("AROW"), AF.Sign, 1.0, ["AROW"], ["CR"])
    select(w("OB"), w("ON"), [[-16, 8], [0, 64]], OP.is_ge, 0.0, 0, 1, ["ON"], ["OB"])
    select(w("OB"), w("OB"), [[16, 8], [0, 64]], OP.is_ge, 0.0, 15, -1, ["OB"], ["OB"])
    for b in range(4): select(w("EB", 512 * b, 512 * b + 512), w("ON"), [[-4, 128], [-1, 4]], OP.is_equal, 0.0, b, 4, ["ON"], ["EB%d" % b])
    iota(w("IOTA"), [[1, 512]], 0, 0, ["IOTA"])
    quant(w("UQ"), w("UQS"), w("UB"), ["UB"], ["UQ"])

    def pick_u(q, o):
        cp(w(q).bitcast(dt.uint32), w("UQ").bitcast(dt.uint32).indirect(w("UO", o, o + 8)), ["UQ", "UO"], [q])
        cp(w(q + "S"), w("UQS").indirect(w("UO", o, o + 8)), ["UQ", "UO"], [q + "S"])

    def later_constants():
        iota(T.CT[0:16, 0:512], [[0, 512]], 1, 0, ["CTx"])
        select(T.CT[0:16, 0:512], T.CT[0:16, 0:512], [[0, 32], [1, 16]], OP.is_gt, 0.0, 0, -1, ["CTx"], ["CTx"])
        select(T.CT[0:16, 0:512], T.CT[0:16, 0:512], [[0, 32], [1, 16]], OP.not_equal, BIG, -1, -1, ["CTx"], ["CTx"])
        iota(T.CT[0:16, 512:544], [[-16, 32]], 511, -1, ["CTy"])
        iota(T.CT[0:16, 544:560], [[16, 16]], 0, 1, ["CTz", "CT0"])
        for i in range(1, 8): dma("y", T.CT[16 * i:16 * i + 16, :], T.CT[0:16, :], "ldc", 7, ["CTx", "CTy", "CTz"], ["CX%d" % i])
        iota(w("I1"), [[1, 512]], 1, 0, ["I1"])
        iota(w("ONEF"), [[0, 256]], 1, 0, ["ONEF"])
        for b in range(4): iota(w("HS", HW * b + 256, HW * b + HW), [[0, 8]], 0, 0, ["HSZ%d" % b])
        iota(w("TRW1"), [[0, 512]], 0, 0, ["TRW1"])

    def turn_rows(t):
        n, lr = "LQK%d" % t, "LR%d" % t
        act(w(n, 0, 128), w(lr).indirect(w("KQ%d" % t, 24, 32)), AF.Copy, 1.0, [lr, "QL%d" % t], [n + "a"])
        act(w(n, 128, 256), w(lr).indirect(w("KQ%d" % t, 16, 24)), AF.Copy, 1.0, [lr, "KL%d" % t], [n + "b"])

    def turn_send(t, back):
        n, tr = "LQK%d" % t, "TR%d" % t
        cp(w(tr).indirect(w("KQ%d" % t, 16, 32)), w(n), [n + "a", n + "b", "QL%d" % t, "KL%d" % t], [tr])
        dma("y", w("TRD%d" % t), T[tr][0:128:16, :], "tro%d" % t, 1, [tr], ["TRD%d" % t])
        send(back, w("TRX%d" % t), w("TRD%d" % t), "tra%d" % t, "trl%d" % t, ["TRD%d" % t])

    def spread(n, src, sem):
        for a in range(16): dma("y", T[n][a:128:16, :], w(src), sem, 16, [src], ["%s.%d" % (n, a)])

    for t in range(ROUNDS):
        d = 2 ** t
        nxt, prv = T.cores[(rank + d) % N], T.cores[(rank - d) % N]
        last = t == ROUNDS - 1
        X, xk = ("X0", ["X0a", "X0b"]) if t == 0 else ("XN%d" % (t - 1), ["XN%d.%d" % (t - 1, b) for b in range(4)])
        xq, xs = w("XQ", 512 * t, 512 * t + 512), w("XS", 512 * t, 512 * t + 512)
        kx = "XQ%d" % t
        ll, lr, kq, br, tb = ("%s%d" % (n, t) for n in ("LL", "LR", "KQ", "BR", "TB"))
        if t == 0: pick_u("UR", 0)
        quant(xq, xs, w(X), xk, [kx])
        if t == 0: pick_u("UT", 8)
        mm(w("P0"), w("UR"), w("URS"), xq, xs, True, True, ["UR", "URS", kx], ["P0"])
        mm(w("P1"), w("UT"), w("UTS"), xq, xs, True, True, ["UT", "UTS", kx], ["P1"])
        if t: turn_send(t - 1, T.cores[(rank - d // 2) % N])
        act(w("BS"), w("P1"), AF.Sign, 1.0, ["P1"], ["BS"])
        actb(w(br), w("BS"), AF.Sign, -0.5, 1.0, ["BS"], [br])
        tt(w("MSK", 0, 512), w("P0"), w("M1"), OP.mult, ["P0", "M1"], ["MSK"])
        tt(w("SBD"), w("P0"), w("MX"), OP.min, ["P0", "MX"], ["SBD"])
        scan(w("SCN"), w("CN"), w("MSK"), ["CN", "CNp", "MSK", "MSKp"], ["SCN"])
        dma("y", w("BRD%d" % t), T[br][0:128:16, :], "bro%d" % t, 1, [br], ["BRD%d" % t])
        send(prv, w("BRX%d" % t), w("BRD%d" % t), "bra%d" % t, "brl%d" % t, ["BRD%d" % t])
        if t:
            p = t - 1
            lands(T.cores[(rank + d // 2) % N], "TRX%d" % p, "tra%d" % p)
            spread("TRW%d" % p, "TRX%d" % p, "trx%d" % p)
        lands(nxt, "BRX%d" % t, "bra%d" % t)
        spread(tb, "BRX%d" % t, "tbx%d" % t)
        if t == 0: later_constants()
        iota(w("EW"), [[0, 512]], 256, 0, ["EW"])

        def colsum(k):
            q, s = w("QT", TO[k], TO[k + 1]), w("QS", TO[k], TO[k + 1])
            quant(q, s, w("BT", 4 * TO[k], 4 * TO[k + 1]), ["BT%d.%d" % (k, i) for i in range(4)] + ["BT%dd" % k], ["QT%d" % k])
            mm(w("P6", 0, TC[k]), w("OQ"), w("OQS"), q, s, k == 7, k == 0, ["OQ", "QT%d" % k], ["P6"])

        for k in range(7, -1, -1):
            o = 4 * TO[k]
            for i in range(3, -1, -1):
                c = 4 * k + i
                key = "BT%d.%d" % (k, i)
                sc = w("SCN", 16 * c + 15, 16 * c + 16)
                if c:
                    ts(w("BT", o + i, o + 64 * c, 4), w("P0", 0, 16 * c), sc, None, OP.is_ge, None, ["P0", "SCN"], [key])
                    j = 8 * c * (c - 1)
                    op("s", lambda: S.activation(w("JUNK", j, j + 16 * c), w("BT", o + i, o + 64 * c, 4), AF.Copy, accum_out=w("RS", c, c + 1)), [key], ["JUNK%d" % c, "RS%d" % c])
                if i == 3:
                    tt(w("BT", o + 256 * k, o + 256 * k + 256, 4), w("SBD", 64 * k, 64 * k + 64), w("SCN", 64 * k + 16, 64 * k + 80), OP.is_ge, ["SBD", "SCN"], ["BT%dd" % k])
                    if k < 7: colsum(k + 1)
                if i == 1: scan(w("DS", 64 * k, 64 * k + 64), w("CR", 64 * k, 64 * k + 64), w("BT", o + 256 * k, o + 256 * k + 256, 4), ["CR", "BT%dd" % k], ["DS%d" % k])
            if k == 7 and t == 0:
                quant(w("OQ"), w("OQS"), w("OB"), ["OB"], ["OQ"])
                cp(w("LL0"), w("LINKI"), ["LINKI"], ["LL0"])
            if k == 6 and t == 0:
                quant(w("EQ"), w("EQS"), w("EB"), ["EB%d" % b for b in range(4)], ["EQ"])
                ts(w("MC"), pm, 15.0, 1.0 - 1.0 / BIG, OP.is_equal, OP.mult, ["PM"], ["MC"])
            if k == 7 and t or k == 6 and not t:
                for b in range(4):
                    mm(w("P%d" % (2 + b)), w("EQ", 128 * b, 128 * b + 128), w("EQS", 128 * b, 128 * b + 128), xq, xs, True, True, ["EQ", kx], ["P%d" % (2 + b)])
            if k == 5:
                if t == 0: ts(w("MC"), w("MC"), 1.0 / BIG, None, OP.add, None, ["MC"], ["MC"])
                if t == 0: act(w(lr), w("IOTA").indirect(w(ll)), AF.Copy, 1.0, ["IOTA", ll], [lr])
            if k == 3:
                if t: act(w(lr), w("TRW%d" % (t - 1)).indirect(w("LL%d" % (t - 1))), AF.Copy, 1.0, ["TRW%d.%d" % (t - 1, a) for a in range(16)] + ["LL%d" % (t - 1)], [lr])
                tt(w("OWS"), w(br), w("I1"), OP.mult, [br, "I1"], ["OWS"])
            if k == 1 and t: lift("EXL", 0, w(lr), 512, lr)
        if t: down(w(ll), "EXL", 0, 512, None, ll)
        else: quant(w("VQ"), w("VQS"), w("VB"), ["VB"], ["VQ"])
        colsum(0)
        for b in range(4): act(w("FH", 512 * b, 512 * b + 512), w("P%d" % (2 + b)), AF.Copy, 0.5, ["P%d" % (2 + b)], ["FH%d" % b])
        act(w("TR%d" % t), w(lr), AF.Copy, 1.0, [lr], ["TR%d" % t])
        tt(w("RSJ"), w("DS", 15, 512, 16), w("R5"), OP.add, ["DS%d" % c for c in range(8)] + CXK, ["RSJ"])
        tt(w("PAY"), w(tb).indirect(w(ll)), w("OWS"), OP.mult, ["%s.%d" % (tb, a) for a in range(16)] + [ll, "OWS"], ["PAY"])
        lift("EXA", 0, w("P6"), 512, "P6")
        tt(w("RSI"), w("RS"), w("RSJ"), OP.add, ["RS%d" % c for c in range(32)] + ["RSJ"], ["RSI"])
        down(w("CSL"), "EXA", 0, 512, None, "CSL")
        tt(w("RK"), w("RSI"), w("CSL"), OP.subtract, ["RSI", "CSL"], ["RK"])
        cp(w("RKU"), w("RK"), ["RK"], ["RKU"])
        cp(w("POS").indirect(w("RKU")), w("PAY"), ["RKU", "PAY"], ["POS"])
        act(w("POSA"), w("POS"), AF.Abs, 1.0, ["POS"], ["POSA"])
        ts(w("FR"), w("POS", 1, 512, 2), 0.0, None, OP.is_lt, None, ["POS"], ["FR"])
        ts(w("F5"), w("POS", 1, 512, 2), 0.0, 512.0, OP.is_lt, OP.mult, ["POS"], ["F5"])
        scan(w("FC"), w("ONEF"), w("FR"), ["ONEF", "FR"], ["FC"])
        tt(w("VP"), w("FC"), w("F5"), OP.add, ["FC", "F5"], ["VP"])
        ts(w("TOT"), w("FC", 255, 256), -1.0, -257.0, OP.mult, OP.add, ["FC"], ["TOT"])
        lift("EXB", 0, w("VP"), 256, "VP")
        down(w("VL"), "EXB", 0, 256, None, "VL")
        tt(w("NX1"), w("J16"), w("VL"), OP.subtract, CXK + ["VL"], ["NX1"])
        ts(w("NX2"), w("VL"), w("TOT"), None, OP.add, None, ["VL", "TOT"], ["NX2"])
        tt(w("NN"), w("NX1"), w("NX2"), OP.max, ["NX1", "NX2"], ["NN"])
        cp(w("NU"), w("NN"), ["NN"], ["NU"])
        cp(w("FO", 0, 256).indirect(w("NU")), w("POSA", 0, 512, 2), ["NU", "POSA"], ["FOk"])
        cp(w("FO", 256, 512).indirect(w("NU")), w("POSA", 1, 512, 2), ["NU", "POSA"], ["FOq"])
        for b in range(4): act(w("FB", 512 * b, 512 * b + 512), w("P%d" % (2 + b)), AF.Copy, 1.0, ["P%d" % (2 + b)], ["FB%d" % b])

        def lists(h):
            o = 128 if h == "L" else 0
            lift("EXK", o, w("FO", o, o + 128), 128, "FOk")
            lift("EXK", o + 256, w("FO", o + 256, o + 384), 128, "FOq")
            down(w(kq, o // 8, o // 8 + 8), "EXK", o, 128, -1.0, "K%s%d" % (h, t))
            down(w(kq, o // 8 + 8, o // 8 + 16), "EXK", o + 256, 128, -1.0, "Q%s%d" % (h, t))

        def firsts(h):
            o, i = (16, 512) if h == "L" else (0, 0)
            for b in range(4):
                act(w("KB", i + 128 * b, i + 128 * b + 128), w("FH", 512 * b, 512 * b + 512).indirect(w(kq, o, o + 8)), AF.Copy, 1.0, ["FH%d" % b, "K%s%d" % (h, t)], ["KB%s%d" % (h, b)])

        def second(h, b):
            o, i = (24, 512) if h == "L" else (8, 0)
            tt(w("A%s%d" % (h, t), b, 512, 4), w("FH", 512 * b, 512 * b + 512).indirect(w(kq, o, o + 8)), w("KB", i + 128 * b, i + 128 * b + 128), OP.add, ["FH%d" % b, "Q%s%d" % (h, t), "KB%s%d" % (h, b)], ["A%s%d.%d" % (h, t, b)])

        def pack(h):
            quant(w("A%sQ%d" % (h, t)), w("A%sS%d" % (h, t)), w("A%s%d" % (h, t)), ["A%s%d.%d" % (h, t, b) for b in range(4)], ["A%sQ%d" % (h, t)])

        lists("K")
        firsts("K")
        cp(w("NMR"), w(lr).indirect(w(kq, 8, 16)), [lr, "QK%d" % t], ["NMR"])
        second("K", 0)
        lift("EXN", 0, w("NMR"), 128, "NMR")
        second("K", 1)
        down(w("NL%d" % t), "EXN", 0, 128, None, "NL%d" % t)
        second("K", 2)
        second("K", 3)
        pack("K")
        send(nxt, w("NLI%d" % t), w("NL%d" % t), "nma%d" % t, "nml%d" % t, ["NL%d" % t])
        send(nxt, w("INQ%d" % t).bitcast(dt.uint8), w("AKQ%d" % t).bitcast(dt.uint8), "cda%d" % t, "cdl%d" % t, ["AKQ%d" % t], 2)
        send(nxt, w("INS%d" % t), w("AKS%d" % t), "cda%d" % t, "cdl%d" % t, ["AKQ%d" % t], 2)
        lists("L")
        if last: turn_rows(t)
        firsts("L")
        if last: turn_send(t, prv)
        for b in range(4): second("L", b)
        pack("L")
        lands(prv, "NLI%d" % t, "nma%d" % t)
        lands(prv, "INQ%d" % t, "cda%d" % t, 2)

        def layer(b, P, q, s, key, o, h):
            mm(w(P, 0, 128), w("WQ", 128 * b, 128 * b + 128), w("WS", 128 * b, 128 * b + 128), w(q), w(s), True, True, ["WQ", "WS", key], [P])
            act(w("HS", HW * b + o, HW * b + o + 128), w(P, 0, 128), AF.Copy, 0.03125, [P], ["HS%d%s" % (b, h)])

        for b in range(4): layer(b, "P%d" % (0, 1, 6, 7)[b], "ALQ%d" % t, "ALS%d" % t, "ALQ%d" % t, 128, "L")
        cp(w("EW").indirect(w(kq, 24, 32)), w("IOTA", 128, 256), ["QL%d" % t, "IOTA"], ["EW"])
        cp(w("EW").indirect(w("NLI%d" % t)), w("IOTA", 0, 128), ["NLI%d" % t, "IOTA"], ["EW"])
        lift("EXE", 0, w("EW"), 512, "EW")
        down(w("EL"), "EXE", 0, 512, None, "EL")
        for b in range(4): layer(b, "P%d" % (2 + b), "INQ%d" % t, "INS%d" % t, "INQ%d" % t, 0, "K")
        for b in range(4):
            tt(w("XN%d" % t, b, 2048, 4), w("HS", HW * b, HW * b + HW).indirect(w("EL")), w("FB", 512 * b, 512 * b + 512), OP.add, ["HS%dK" % b, "HS%dL" % b, "HSZ%d" % b, "EL", "FB%d" % b], ["XN%d.%d" % (t, b)])
        if not last: turn_rows(t)

    t = ROUNDS - 1
    lands(T.cores[(rank + 2 ** t) % N], "TRX%d" % t, "tra%d" % t)
    dma("y", T["TRW%d" % t][0:128:16, :], w("TRX%d" % t), "trx%d" % t, 1, ["TRX%d" % t], ["TRW%d" % t])
    stores, e = 13, 512 * ROUNDS
    for h in range(2):
        o = e + 256 * h
        quant(w("XQ", o, o + 256), w("XS", o, o + 256), w("XN%d" % t, 1024 * h, 1024 * h + 1024), ["XN%d.%d" % (t, b) for b in range(4)], ["XQe%d" % h])
        mm(w("P%d" % (6 + h), 0, 256), w("VQ"), w("VQS"), w("XQ", o, o + 256), w("XS", o, o + 256), True, True, ["VQ", "XQe%d" % h], ["P%d" % (6 + h)])
        dma("y", T.oc[:, 1024 * h:1024 * h + 1024], w("XQ", o, o + 256).bitcast(dt.uint8), "st", stores, ["XQe%d" % h], ["oc%d" % h])
    act(w("YS", 0, 256), w("P6", 0, 256), AF.Copy, 1.0, ["P6"], ["YSa"])
    cp(w("YS", 256, 512), w("P7", 0, 256), ["P7"], ["YSb"])
    dma("s", T.y[:, 0:256], w("YS", 0, 256), "st", stores, ["YSa"], ["ya"])
    dma("y", T.y[:, 256:512], w("YS", 256, 512), "st", stores, ["YSb"], ["yb"])
    act(w("LKO"), w("TRW%d" % t).indirect(w("LL%d" % t)), AF.Copy, 1.0, ["TRW%d" % t, "LL%d" % t], ["LKO"])
    dma("s", T.lk[:, :], T.LKO[0:128:16, :], "st", stores, ["LKO"], ["lk"])
    for k in range(4):
        for h in range(2):
            o = e + 256 * h
            dma("y", T.osc[4 * k:4 * k + 4, 256 * h:256 * h + 256], T.XS[32 * k:32 * k + 4, o:o + 256], "st", stores, ["XQe%d" % h], ["osc%d%d" % (k, h)])
    for sem in total:
        if know["g"].get(sem, 0) < total[sem]: g.wait_ge(T.sem[sem], total[sem])
